import numpy as np
import ml_dtypes


def mxq(x, axis, fmt="e4m3"):
    dtype, down = {"e4m3": (ml_dtypes.float8_e4m3fn, 7), "e5m2": (ml_dtypes.float8_e5m2, 14)}[fmt]
    v = np.moveaxis(np.asarray(x, np.float32).astype(ml_dtypes.bfloat16).astype(np.float64), axis, -1)
    blocks = v.reshape(v.shape[:-1] + (-1, 32))
    amax = np.abs(blocks).max(-1, keepdims=True)
    byte = np.maximum(np.where(amax > 0, np.frexp(amax)[1] - 1 + 127, 0) - down, 1)
    scale = np.exp2(byte - 127.0)
    codes = (blocks / scale).astype(np.float32).astype(dtype).astype(np.float64)
    return np.moveaxis((codes * scale).reshape(v.shape), -1, axis)


WIDE = False


def mx_kscale(k):
    if not WIDE:
        return np.ones(k)
    levels = np.array([18, -18])
    if k % 512:
        return np.exp2(np.random.permutation(np.resize(levels, k // 32))).repeat(32)
    a = np.empty((k // 512, 16))
    for p in range(k // 512):
        a[p, :8] = np.random.permutation(np.resize(levels, 8))
        for g in range(8):
            far = levels[np.abs(levels - a[p, g]) >= 10]
            a[p, g + 8] = far[np.random.randint(len(far))]
    return np.exp2(a.ravel()).repeat(32)


def f64(x):
    return np.asarray(x).astype(np.float64)


def striped(idx):
    return np.tile(np.asarray(idx).reshape(-1, 16).T, (8, 1)).astype(np.uint16)


def unstriped(offs):
    return offs[:16].T.reshape(-1).astype(np.int64)


E2M1 = np.array([0.0, 0.5, 1.0, 1.5, 2.0, 3.0, 4.0, 6.0, -0.0, -0.5, -1.0, -1.5, -2.0, -3.0, -4.0, -6.0])


def pack_weight(w, fmt):
    k, n = w.shape
    w = f64(np.asarray(w, np.float32).astype(ml_dtypes.bfloat16)).reshape(k // 32, 32, n)
    amax = np.abs(w).max(1)
    if fmt == "e4m3":
        byte = np.frexp(amax)[1] - 1 + 127 - 7
    else:
        mant, ex = np.frexp(amax / 6.0)
        byte = np.where(mant > 0.5, ex, ex - 1) + 127
    byte = np.clip(np.where(amax > 0, byte, 1), 1, 254)
    scaled = (w * np.exp2(127.0 - byte)[:, None, :]).reshape(k, n).astype(np.float32)
    by_word = np.ascontiguousarray(scaled.reshape(k // 512, 128, 4, n).transpose(0, 1, 3, 2))
    if fmt == "e4m3":
        words = by_word.astype(ml_dtypes.float8_e4m3fn).view(np.uint8)
    else:
        c = by_word.astype(ml_dtypes.float4_e2m1fn).view(np.uint8) & 0xF
        words = (c[..., 0::2] | (c[..., 1::2] << 4)).reshape(k // 512, 128, 2 * n)
    return np.ascontiguousarray(words), np.ascontiguousarray(byte.astype(np.uint8).reshape(k // 512, 16, n))


def unpack_weight(words, scales, fmt):
    g, _, n = scales.shape
    words = np.ascontiguousarray(words).reshape(g, 128, n, -1)
    if fmt == "e4m3":
        vals = words.view(ml_dtypes.float8_e4m3fn).astype(np.float64)
    else:
        nib = np.empty((g, 128, n, 4), np.uint8)
        nib[..., 0::2] = words & 0xF
        nib[..., 1::2] = words >> 4
        vals = E2M1[nib]
    vals = vals * np.repeat(np.exp2(scales.astype(np.float64) - 127.0), 8, axis=1)[..., None]
    return vals.transpose(0, 1, 3, 2).reshape(g * 512, n)


B, N, T, D, R = 1, 512, 2048, 1024, 512


def setup_inputs():
    n = np.random.standard_normal
    idx = np.random.permutation(T)[:B * N]
    s = mx_kscale(D)[:, None]
    z = mx_kscale(R)[:, None]
    x = n((B, D, R))
    vp = pack_weight(n((D, T)) / np.sqrt(D) / s, "e2m1")
    return {
        "xT": (x * s).astype(np.float32),
        "wT": (n((D, T)) * (1.00 / np.sqrt(D)) / s).astype(np.float32),
        "v_words": np.ascontiguousarray(vp[0].reshape(1, 2, 128, T, 2).transpose(0, 2, 3, 1, 4)).reshape(1, 128, T, 4),
        "v_scales": vp[1],
        "wt": (np.random.uniform(0.5, 1.5, (B, R, 1)) * 1.0 / np.sqrt(R) * z).astype(np.float32),
        "xm": (x.transpose(0, 2, 1) / z).astype(np.float32),
        "offs": striped(idx),
    }


def reference(xT, wT, v_words, v_scales, wt, xm, offs):
    idx = unstriped(offs)
    v = unpack_weight(v_words.reshape(1, 128, T, 2, 2).transpose(0, 3, 1, 2, 4).reshape(2, 128, 2 * T), v_scales, "e2m1")
    pick = lambda x: x[:, idx].reshape(x.shape[0], B, N).transpose(1, 0, 2)
    xq = mxq(f64(xT), 1, "e4m3").transpose(0, 2, 1)
    a = xq @ mxq(pick(f64(wT)), 1, "e4m3")
    av = xq @ pick(v)
    g = f64(wt) * (1.0 / (1.0 + np.exp(-a)) - 1.0 / (1.0 + np.exp(-av)))
    dw = mxq(f64(xm), 1, "e4m3").transpose(0, 2, 1) @ mxq(g, 1, "e5m2")
    gw = np.zeros((D, T))
    gw[:, idx] = dw.transpose(1, 0, 2).reshape(D, B * N)
    return gw

@@ -1,0 +1,221 @@
+from contextlib import ExitStack
+
+import concourse.mybir as mybir
+from concourse.masks import make_identity
+
+D, T, N, R = 1024, 2048, 512, 512
+FLOPS = 3 * 2 * D * N * R
+
+F32 = mybir.dt.float32
+BF16 = mybir.dt.bfloat16
+I32 = mybir.dt.int32
+U32 = mybir.dt.uint32
+U16 = mybir.dt.uint16
+U8 = mybir.dt.uint8
+E4M3 = mybir.dt.float8_e4m3fn_x4
+E5M2 = mybir.dt.float8_e5m2_x4
+E2M1 = mybir.dt.float4_e2m1fn_x4
+TANH = mybir.ActivationFunctionType.Tanh
+MULT = mybir.AluOpType.mult
+
+P = 128
+PACK = 4
+K_PASS = P * PACK
+PASSES = D // K_PASS
+HALF = N // 2
+SLOT_TILES = N // P
+WINDOWS = 3
+XM_WIDTHS = (128, 128, 256, 512)
+PLANES_BEFORE_TEACHER = 5
+
+
+def interleave(nc, grouped, raw):
+    nc.scalar.copy(
+        out=grouped[:].rearrange("p (c i) t -> p c t i", i=PACK),
+        in_=raw.rearrange("p t (c i) -> p c t i", i=PACK),
+    )
+
+
+def quantize(nc, codes, scales, grouped, fmt):
+    nc.vector.quantize_mx(out=codes.bitcast(fmt), scales=scales, in_=grouped.rearrange("p c t -> p (c t)"))
+
+
+def tile_attend_gds_nce_kernel(tc, xT, wT, v_words, v_scales, wt, xm, offs, out):
+    nc = tc.nc
+    with ExitStack() as ctx:
+        held = ctx.enter_context(tc.tile_pool(name="held", bufs=1))
+        psum = ctx.enter_context(tc.psum_pool(name="psum", bufs=1))
+
+        def sb(name, shape, dtype):
+            return held.tile(shape, dtype, name=name, align_bytes=64)
+
+        offsets = held.tile([P, N // 16], U16, name="offsets")
+        nc.sync.dma_start(offsets[:], offs)
+        half_lists = [offsets[:, h * (HALF // 16) : (h + 1) * (HALF // 16)] for h in range(2)]
+
+        diff_banks = [psum.tile([P, R], F32, name="diff_bank%d" % q) for q in range(SLOT_TILES)]
+        score_banks = [psum.tile([P, R], F32, name="score_bank%d" % q) for q in range(SLOT_TILES)]
+
+        v_scale_table = sb("v_scale_table", [P, PASSES * T], U8)
+        nc.vector.memset(v_scale_table[:].bitcast(I32), 0)
+        windows = [sb("window%d" % i, [P, T], F32) for i in range(WINDOWS)]
+        for window in windows:
+            nc.vector.memset(window[:], 0.0)
+        identity = sb("identity", [P, P], F32)
+        make_identity(nc, identity[:])
+        row_weights = sb("row_weights", [P, PACK], F32)
+        nc.scalar.dma_start(row_weights[:], wt[0].rearrange("(p j) o -> p (j o)", j=PACK))
+        for quad in range(4):
+            nc.scalar.dma_start(
+                v_scale_table[32 * quad : 32 * quad + 4, :].bitcast(I32).rearrange("f (o t) -> f o t", o=PASSES),
+                v_scales[:, 4 * quad : 4 * quad + 4, :].bitcast(I32).rearrange("o f t -> f o t"),
+            )
+
+        w_planes = [sb("w_plane%d" % i, [P, T], F32) for i in range(PASSES * PACK)]
+        x_raw = [sb("x_raw%d" % g, [P, PACK, R], F32) for g in range(PASSES)]
+        v_table = sb("v_table", [P, T], U32)
+        w_rows = wT.rearrange("(g p t) c -> g t p c", p=P, t=PACK)
+        for i, plane in enumerate(w_planes):
+            if i == PLANES_BEFORE_TEACHER:
+                nc.sync.dma_start(v_table[:].bitcast(I32), v_words[0].rearrange("p t b -> p (t b)").bitcast(I32))
+            nc.sync.dma_start(plane[:], w_rows[i // PACK, i % PACK])
+            if i < PASSES:
+                rows = xT[0, i * K_PASS : (i + 1) * K_PASS, :]
+                nc.sync.dma_start(x_raw[i][:], rows.rearrange("(p t) r -> p t r", t=PACK))
+        xm_rows = xm[0].rearrange("(p t) d -> p t d", t=PACK)
+        xm_raw = []
+        first = 0
+        for c, width in enumerate(XM_WIDTHS):
+            raw = sb("xm_raw%d" % c, [P, PACK, width], F32)
+            nc.sync.dma_start(raw[:], xm_rows[:, :, first : first + width])
+            xm_raw.extend(raw[:, :, u * P : (u + 1) * P] for u in range(width // P))
+            first = first + width
+
+        x_codes, x_scales = [], []
+        for g in range(PASSES):
+            grouped = sb("x_grouped%d" % g, [P, R, PACK], BF16)
+            interleave(nc, grouped, x_raw[g][:])
+            x_codes.append(sb("x_codes%d" % g, [P, R], U32))
+            x_scales.append(sb("x_scales%d" % g, [P, R], U8))
+            quantize(nc, x_codes[g][:], x_scales[g][:], grouped[:], E4M3)
+
+        v_slot_scales = sb("v_slot_scales", [P, PASSES, N], U8)
+        for g in range(PASSES):
+            nc.vector.tensor_copy(v_slot_scales[:, g, :], v_scale_table[:, g * T : (g + 1) * T].indirect(offsets[:]))
+
+        w_grouped = [[sb("w_grouped%d_%d" % (g, h), [P, HALF, PACK], BF16) for h in range(2)] for g in range(PASSES)]
+
+        def gather_plane(i, h):
+            nc.vector.tensor_copy(w_grouped[i // PACK][h][:, :, i % PACK], w_planes[i][:].indirect(half_lists[h]))
+
+        w_codes = [[sb("w_codes%d_%d" % (g, h), [P, HALF], U32) for h in range(2)] for g in range(PASSES)]
+        w_scales = [[sb("w_scales%d_%d" % (g, h), [P, HALF], U8) for h in range(2)] for g in range(PASSES)]
+
+        def student_pass(g, h):
+            codes, scales = w_codes[g][h], w_scales[g][h]
+            for u in range(2):
+                cols = slice(u * P, (u + 1) * P)
+                nc.tensor.matmul_mx(
+                    out=score_banks[2 * h + u][:],
+                    lhsT=codes[:, cols].bitcast(E4M3),
+                    lhsT_scale=scales[:, cols],
+                    rhs=x_codes[g][:].bitcast(E4M3),
+                    rhs_scale=x_scales[g][:],
+                    start=(g == 0),
+                    stop=(g == PASSES - 1),
+                )
+
+        def tanh_and_turn(name, q, scores, scale, opens):
+            halves = sb("%s_tanh%d" % (name, q), [P, PACK, P], F32)
+            nc.scalar.activation(halves[:], scores[:].rearrange("p (s j) -> p j s", j=PACK), TANH, scale=scale)
+            for j in range(PACK):
+                nc.tensor.matmul(
+                    diff_banks[q][:, j * P : (j + 1) * P],
+                    lhsT=halves[:, j, :],
+                    rhs=identity[:],
+                    is_transpose=True,
+                    start=(opens and j == 0),
+                    stop=(not opens and j == PACK - 1),
+                )
+
+        def teacher():
+            v_codes = []
+            for h in range(2):
+                v_pairs = sb("v_pairs%d" % h, [P, HALF], U32)
+                nc.vector.tensor_copy(v_pairs[:], v_table[:].indirect(half_lists[h]))
+                v_codes.append(sb("v_codes%d" % h, [P, PASSES, HALF], U16))
+                nc.vector.tensor_copy(v_codes[h][:], v_pairs[:].bitcast(U16).rearrange("p (n o) -> p o n", o=PASSES))
+            for q in range(SLOT_TILES):
+                cols = slice(q * P, (q + 1) * P)
+                half_cols = slice((q % 2) * P, (q % 2 + 1) * P)
+                for g in range(PASSES):
+                    nc.tensor.matmul_mx(
+                        out=score_banks[q][:],
+                        lhsT=v_codes[q // 2][:, g, half_cols].bitcast(E2M1),
+                        lhsT_scale=v_slot_scales[:, g, cols],
+                        rhs=x_codes[g][:].bitcast(E4M3),
+                        rhs_scale=x_scales[g][:],
+                        start=(g == 0),
+                        stop=(g == PASSES - 1),
+                    )
+            for q in range(SLOT_TILES):
+                tanh_and_turn("teacher", q, score_banks[q], -0.5, True)
+
+        for i in range(PASSES * PACK):
+            if i == PLANES_BEFORE_TEACHER:
+                teacher()
+                for h in range(2):
+                    student_pass(0, h)
+            for h in range(2):
+                gather_plane(i, h)
+                if i % PACK == PACK - 1:
+                    g = i // PACK
+                    quantize(nc, w_codes[g][h][:], w_scales[g][h][:], w_grouped[g][h][:], E4M3)
+        for h in range(2):
+            student_pass(1, h)
+
+        xm_codes = [sb("xm_codes%d" % m, [P, P], U32) for m in range(D // P)]
+        xm_scales = [sb("xm_scales%d" % m, [P, P], U8) for m in range(D // P)]
+
+        def quantize_xm(m):
+            grouped = sb("xm_grouped%d" % m, [P, P, PACK], BF16)
+            interleave(nc, grouped, xm_raw[m])
+            quantize(nc, xm_codes[m][:], xm_scales[m][:], grouped[:], E4M3)
+
+        quantize_xm(0)
+
+        g_codes = sb("g_codes", [P, N], U32)
+        g_scales = sb("g_scales", [P, N], U8)
+        for q in range(SLOT_TILES):
+            tanh_and_turn("student", q, score_banks[q], 0.5, False)
+            g_grouped = sb("g_grouped%d" % q, [P, P, PACK], BF16)
+            nc.vector.scalar_tensor_tensor(
+                out=g_grouped[:],
+                in0=diff_banks[q][:].rearrange("p (j n) -> p n j", j=PACK),
+                scalar=0.5,
+                in1=row_weights[:].unsqueeze(1).to_broadcast([P, P, PACK]),
+                op0=MULT,
+                op1=MULT,
+            )
+            cols = slice(q * P, (q + 1) * P)
+            quantize(nc, g_codes[:, cols], g_scales[:, cols], g_grouped[:], E5M2)
+
+        for m in range(D // P):
+            bank = score_banks[m % SLOT_TILES]
+            nc.tensor.matmul_mx(
+                out=bank[:],
+                lhsT=xm_codes[m][:].bitcast(E4M3),
+                lhsT_scale=xm_scales[m][:],
+                rhs=g_codes[:].bitcast(E5M2),
+                rhs_scale=g_scales[:],
+                start=True,
+                stop=True,
+            )
+            dw = sb("dw%d" % m, [P, N], F32)
+            nc.scalar.copy(out=dw[:], in_=bank[:])
+            window = windows[m % WINDOWS]
+            nc.vector.tensor_copy(window[:].indirect(offsets[:]), dw[:])
+            nc.sync.dma_start(out[m * P : (m + 1) * P, :], window[:])
+            if m == 0:
+                for later in range(1, D // P):
+                    quantize_xm(later)

@@ -24,14 +24,13 @@ K_PASS = P * PACK
 PASSES = D // K_PASS
 HALF = N // 2
 SLOT_TILES = N // P
-WINDOWS = 3
-XM_WIDTHS = (128, 128, 256, 512)
-PLANES_BEFORE_TEACHER = 5
+WINDOWS = 4
+XM_LOADS = (128, 384, 512)
 
 
 def interleave(nc, grouped, raw):
     nc.scalar.copy(
-        out=grouped[:].rearrange("p (c i) t -> p c t i", i=PACK),
+        out=grouped.rearrange("p (c i) t -> p c t i", i=PACK),
         in_=raw.rearrange("p t (c i) -> p c t i", i=PACK),
     )
 
@@ -46,11 +45,10 @@ def tile_attend_gds_nce_kernel(tc, xT, wT, v_words, v_scales, wt, xm, offs, out)
         held = ctx.enter_context(tc.tile_pool(name="held", bufs=1))
         psum = ctx.enter_context(tc.psum_pool(name="psum", bufs=1))
 
-        def sb(name, shape, dtype):
-            return held.tile(shape, dtype, name=name, align_bytes=64)
+        def sb(name, shape, dtype, tag=None):
+            return held.tile(shape, dtype, name=name, tag=tag or name, align_bytes=64)
 
         offsets = held.tile([P, N // 16], U16, name="offsets")
-        nc.sync.dma_start(offsets[:], offs)
         half_lists = [offsets[:, h * (HALF // 16) : (h + 1) * (HALF // 16)] for h in range(2)]
 
         diff_banks = [psum.tile([P, R], F32, name="diff_bank%d" % q) for q in range(SLOT_TILES)]
@@ -59,33 +57,39 @@ def tile_attend_gds_nce_kernel(tc, xT, wT, v_words, v_scales, wt, xm, offs, out)
         v_scale_table = sb("v_scale_table", [P, PASSES * T], U8)
         nc.vector.memset(v_scale_table[:].bitcast(I32), 0)
         windows = [sb("window%d" % i, [P, T], F32) for i in range(WINDOWS)]
-        for window in windows:
-            nc.vector.memset(window[:], 0.0)
+        g_codes = sb("g_codes", [P, HALF + N], U32)
+        g_scales = sb("g_scales", [P, HALF + N], U8)
         identity = sb("identity", [P, P], F32)
         make_identity(nc, identity[:])
         row_weights = sb("row_weights", [P, PACK], F32)
         nc.scalar.dma_start(row_weights[:], wt[0].rearrange("(p j) o -> p (j o)", j=PACK))
+
+        w_rows = wT.rearrange("(g p t) c -> g t p c", p=P, t=PACK)
+        x_rows = xT[0].rearrange("(g p t) r -> g p t r", p=P, t=PACK)
+        w_planes = [[sb("w_plane%d_%d" % (g, t), [P, T], F32) for t in range(PACK)] for g in range(PASSES)]
+        x_raw = [sb("x_raw%d" % g, [P, PACK, R], F32) for g in range(PASSES)]
+        v_table = sb("v_table", [P, T], U32)
+        nc.sync.dma_start(w_planes[0][0][:], w_rows[0, 0])
+        nc.sync.dma_start(offsets[:], offs)
         for quad in range(4):
-            nc.scalar.dma_start(
+            nc.sync.dma_start(
                 v_scale_table[32 * quad : 32 * quad + 4, :].bitcast(I32).rearrange("f (o t) -> f o t", o=PASSES),
                 v_scales[:, 4 * quad : 4 * quad + 4, :].bitcast(I32).rearrange("o f t -> f o t"),
             )
-
-        w_planes = [sb("w_plane%d" % i, [P, T], F32) for i in range(PASSES * PACK)]
-        x_raw = [sb("x_raw%d" % g, [P, PACK, R], F32) for g in range(PASSES)]
-        v_table = sb("v_table", [P, T], U32)
-        w_rows = wT.rearrange("(g p t) c -> g t p c", p=P, t=PACK)
-        for i, plane in enumerate(w_planes):
-            if i == PLANES_BEFORE_TEACHER:
-                nc.sync.dma_start(v_table[:].bitcast(I32), v_words[0].rearrange("p t b -> p (t b)").bitcast(I32))
-            nc.sync.dma_start(plane[:], w_rows[i // PACK, i % PACK])
-            if i < PASSES:
-                rows = xT[0, i * K_PASS : (i + 1) * K_PASS, :]
-                nc.sync.dma_start(x_raw[i][:], rows.rearrange("(p t) r -> p t r", t=PACK))
+        for u in range(2):
+            nc.sync.dma_start(x_raw[0][:, 2 * u : 2 * u + 2, :], x_rows[0, :, 2 * u : 2 * u + 2, :])
+        nc.sync.dma_start(w_planes[0][1][:], w_rows[0, 1])
+        for u in range(2):
+            nc.sync.dma_start(x_raw[1][:, 2 * u : 2 * u + 2, :], x_rows[1, :, 2 * u : 2 * u + 2, :])
+        nc.sync.dma_start(v_table[:].bitcast(I32), v_words[0].rearrange("p t b -> p (t b)").bitcast(I32))
+        for t in range(2, PACK):
+            nc.sync.dma_start(w_planes[0][t][:], w_rows[0, t])
+        for t in range(PACK):
+            nc.sync.dma_start(w_planes[1][t][:], w_rows[1, t])
         xm_rows = xm[0].rearrange("(p t) d -> p t d", t=PACK)
         xm_raw = []
         first = 0
-        for c, width in enumerate(XM_WIDTHS):
+        for c, width in enumerate(XM_LOADS):
             raw = sb("xm_raw%d" % c, [P, PACK, width], F32)
             nc.sync.dma_start(raw[:], xm_rows[:, :, first : first + width])
             xm_raw.extend(raw[:, :, u * P : (u + 1) * P] for u in range(width // P))
@@ -94,7 +98,7 @@ def tile_attend_gds_nce_kernel(tc, xT, wT, v_words, v_scales, wt, xm, offs, out)
         x_codes, x_scales = [], []
         for g in range(PASSES):
             grouped = sb("x_grouped%d" % g, [P, R, PACK], BF16)
-            interleave(nc, grouped, x_raw[g][:])
+            interleave(nc, grouped[:], x_raw[g][:])
             x_codes.append(sb("x_codes%d" % g, [P, R], U32))
             x_scales.append(sb("x_scales%d" % g, [P, R], U8))
             quantize(nc, x_codes[g][:], x_scales[g][:], grouped[:], E4M3)
@@ -105,14 +109,14 @@ def tile_attend_gds_nce_kernel(tc, xT, wT, v_words, v_scales, wt, xm, offs, out)
 
         w_grouped = [[sb("w_grouped%d_%d" % (g, h), [P, HALF, PACK], BF16) for h in range(2)] for g in range(PASSES)]
 
-        def gather_plane(i, h):
-            nc.vector.tensor_copy(w_grouped[i // PACK][h][:, :, i % PACK], w_planes[i][:].indirect(half_lists[h]))
+        def gather_plane(g, t):
+            for h in range(2):
+                nc.vector.tensor_copy(w_grouped[g][h][:, :, t], w_planes[g][t][:].indirect(half_lists[h]))
 
-        w_codes = [[sb("w_codes%d_%d" % (g, h), [P, HALF], U32) for h in range(2)] for g in range(PASSES)]
-        w_scales = [[sb("w_scales%d_%d" % (g, h), [P, HALF], U8) for h in range(2)] for g in range(PASSES)]
-
-        def student_pass(g, h):
-            codes, scales = w_codes[g][h], w_scales[g][h]
+        def student_pass(g, h, tag):
+            codes = sb("w_codes%d_%d" % (g, h), [P, HALF], U32, tag)
+            scales = sb("w_scales%d_%d" % (g, h), [P, HALF], U8)
+            quantize(nc, codes[:], scales[:], w_grouped[g][h][:], E4M3)
             for u in range(2):
                 cols = slice(u * P, (u + 1) * P)
                 nc.tensor.matmul_mx(
@@ -161,61 +165,80 @@ def tile_attend_gds_nce_kernel(tc, xT, wT, v_words, v_scales, wt, xm, offs, out)
             for q in range(SLOT_TILES):
                 tanh_and_turn("teacher", q, score_banks[q], -0.5, True)
 
-        for i in range(PASSES * PACK):
-            if i == PLANES_BEFORE_TEACHER:
-                teacher()
-                for h in range(2):
-                    student_pass(0, h)
-            for h in range(2):
-                gather_plane(i, h)
-                if i % PACK == PACK - 1:
-                    g = i // PACK
-                    quantize(nc, w_codes[g][h][:], w_scales[g][h][:], w_grouped[g][h][:], E4M3)
+        teacher()
+
+        for t in range(PACK):
+            gather_plane(0, t)
+        gather_plane(1, 0)
         for h in range(2):
-            student_pass(1, h)
+            gather_plane(1, 1 + h)
+            student_pass(0, h, "w_plane1_%d" % (1 + h))
+        gather_plane(1, PACK - 1)
+        for h in range(2):
+            student_pass(1, h, None)
 
-        xm_codes = [sb("xm_codes%d" % m, [P, P], U32) for m in range(D // P)]
-        xm_scales = [sb("xm_scales%d" % m, [P, P], U8) for m in range(D // P)]
+        xm_codes, xm_scales = [], []
 
-        def quantize_xm(m):
-            grouped = sb("xm_grouped%d" % m, [P, P, PACK], BF16)
-            interleave(nc, grouped, xm_raw[m])
-            quantize(nc, xm_codes[m][:], xm_scales[m][:], grouped[:], E4M3)
+        def quantize_xm(first, count, tag):
+            grouped = sb("xm_grouped%d" % first, [P, count * P, PACK], BF16, tag)
+            for u in range(count):
+                interleave(nc, grouped[:, u * P : (u + 1) * P, :], xm_raw[first + u])
+            codes = sb("xm_codes%d" % first, [P, count * P], U32)
+            scales = sb("xm_scales%d" % first, [P, count * P], U8)
+            quantize(nc, codes[:], scales[:], grouped[:], E4M3)
+            for u in range(count):
+                xm_codes.append(codes[:, u * P : (u + 1) * P])
+                xm_scales.append(scales[:, u * P : (u + 1) * P])
 
-        quantize_xm(0)
-
-        g_codes = sb("g_codes", [P, N], U32)
-        g_scales = sb("g_scales", [P, N], U8)
-        for q in range(SLOT_TILES):
-            tanh_and_turn("student", q, score_banks[q], 0.5, False)
-            g_grouped = sb("g_grouped%d" % q, [P, P, PACK], BF16)
-            nc.vector.scalar_tensor_tensor(
-                out=g_grouped[:],
-                in0=diff_banks[q][:].rearrange("p (j n) -> p n j", j=PACK),
-                scalar=0.5,
-                in1=row_weights[:].unsqueeze(1).to_broadcast([P, P, PACK]),
-                op0=MULT,
-                op1=MULT,
-            )
-            cols = slice(q * P, (q + 1) * P)
-            quantize(nc, g_codes[:, cols], g_scales[:, cols], g_grouped[:], E5M2)
-
-        for m in range(D // P):
-            bank = score_banks[m % SLOT_TILES]
+        def gradient_product(m, bank, first):
             nc.tensor.matmul_mx(
                 out=bank[:],
-                lhsT=xm_codes[m][:].bitcast(E4M3),
-                lhsT_scale=xm_scales[m][:],
-                rhs=g_codes[:].bitcast(E5M2),
-                rhs_scale=g_scales[:],
+                lhsT=xm_codes[m].bitcast(E4M3),
+                lhsT_scale=xm_scales[m],
+                rhs=g_codes[:, first : first + N].bitcast(E5M2),
+                rhs_scale=g_scales[:, first : first + N],
                 start=True,
                 stop=True,
             )
+
+        quantize_xm(0, 1, None)
+
+        half_weights = sb("half_weights", [P, P, PACK], F32)
+        nc.vector.tensor_scalar_mul(half_weights[:], row_weights[:].unsqueeze(1).to_broadcast([P, P, PACK]), 0.5)
+        first_dw = [sb("first_dw%d" % h, [P, HALF], F32) for h in range(2)]
+        for q in range(SLOT_TILES):
+            tanh_and_turn("student", q, score_banks[q], 0.5, False)
+            g_grouped = sb("g_grouped%d" % q, [P, P, PACK], BF16)
+            nc.vector.tensor_tensor(
+                g_grouped[:], diff_banks[q][:].rearrange("p (j n) -> p n j", j=PACK), half_weights[:], MULT
+            )
+            cols = slice(HALF + q * P, HALF + (q + 1) * P)
+            quantize(nc, g_codes[:, cols], g_scales[:, cols], g_grouped[:], E5M2)
+
+        nc.vector.memset(g_codes[:, :HALF].bitcast(I32), 0)
+        nc.vector.memset(g_scales[:, :HALF].bitcast(I32), 0)
+        for window in windows:
+            nc.vector.memset(window[:], 0.0)
+        gradient_product(0, score_banks[0], 0)
+        nc.scalar.copy(out=first_dw[0][:], in_=score_banks[0][:, HALF:])
+        gradient_product(0, score_banks[1], HALF)
+        nc.scalar.copy(out=first_dw[1][:], in_=score_banks[1][:, HALF:])
+        for h in range(2):
+            nc.vector.tensor_copy(windows[0][:].indirect(half_lists[h]), first_dw[h][:])
+        nc.sync.dma_start(out[0:P, :], windows[0][:])
+
+        def finish(m):
+            bank = score_banks[(m + 1) % SLOT_TILES]
+            gradient_product(m, bank, HALF)
             dw = sb("dw%d" % m, [P, N], F32)
             nc.scalar.copy(out=dw[:], in_=bank[:])
             window = windows[m % WINDOWS]
             nc.vector.tensor_copy(window[:].indirect(offsets[:]), dw[:])
             nc.sync.dma_start(out[m * P : (m + 1) * P, :], window[:])
-            if m == 0:
-                for later in range(1, D // P):
-                    quantize_xm(later)
+
+        quantize_xm(1, 1, "student_tanh0")
+        quantize_xm(2, 2, "student_tanh1")
+        finish(1)
+        quantize_xm(4, 4, "g_grouped%d" % (SLOT_TILES - 1))
+        for m in range(2, D // P):
+            finish(m)

@@ -24,7 +24,7 @@ K_PASS = P * PACK
 PASSES = D // K_PASS
 HALF = N // 2
 SLOT_TILES = N // P
-WINDOWS = 4
+WINDOWS = 3
 XM_LOADS = (128, 384, 512)
 
 
@@ -71,10 +71,10 @@ def tile_attend_gds_nce_kernel(tc, xT, wT, v_words, v_scales, wt, xm, offs, out)
         v_table = sb("v_table", [P, T], U32)
         nc.sync.dma_start(w_planes[0][0][:], w_rows[0, 0])
         nc.sync.dma_start(offsets[:], offs)
-        for quad in range(4):
+        scale_rows = v_scales.bitcast(I32).rearrange("o (q f) t -> f q o t", f=4)
+        for f in range(4):
             nc.sync.dma_start(
-                v_scale_table[32 * quad : 32 * quad + 4, :].bitcast(I32).rearrange("f (o t) -> f o t", o=PASSES),
-                v_scales[:, 4 * quad : 4 * quad + 4, :].bitcast(I32).rearrange("o f t -> f o t"),
+                v_scale_table[f:P:32, :].bitcast(I32).rearrange("q (o t) -> q o t", o=PASSES), scale_rows[f]
             )
         for u in range(2):
             nc.sync.dma_start(x_raw[0][:, 2 * u : 2 * u + 2, :], x_rows[0, :, 2 * u : 2 * u + 2, :])
@@ -109,8 +109,8 @@ def tile_attend_gds_nce_kernel(tc, xT, wT, v_words, v_scales, wt, xm, offs, out)
 
         w_grouped = [[sb("w_grouped%d_%d" % (g, h), [P, HALF, PACK], BF16) for h in range(2)] for g in range(PASSES)]
 
-        def gather_plane(g, t):
-            for h in range(2):
+        def gather_plane(g, t, halves=(0, 1)):
+            for h in halves:
                 nc.vector.tensor_copy(w_grouped[g][h][:, :, t], w_planes[g][t][:].indirect(half_lists[h]))
 
         def student_pass(g, h, tag):
@@ -173,8 +173,8 @@ def tile_attend_gds_nce_kernel(tc, xT, wT, v_words, v_scales, wt, xm, offs, out)
         for h in range(2):
             gather_plane(1, 1 + h)
             student_pass(0, h, "w_plane1_%d" % (1 + h))
-        gather_plane(1, PACK - 1)
         for h in range(2):
+            gather_plane(1, PACK - 1, (h,))
             student_pass(1, h, None)
 
         xm_codes, xm_scales = [], []

@@ -25,7 +25,6 @@ PASSES = D // K_PASS
 HALF = N // 2
 SLOT_TILES = N // P
 WINDOWS = 3
-XM_LOADS = (128, 384, 512)
 
 
 def interleave(nc, grouped, raw):
@@ -66,34 +65,36 @@ def tile_attend_gds_nce_kernel(tc, xT, wT, v_words, v_scales, wt, xm, offs, out)
 
         w_rows = wT.rearrange("(g p t) c -> g t p c", p=P, t=PACK)
         x_rows = xT[0].rearrange("(g p t) r -> g p t r", p=P, t=PACK)
-        w_planes = [[sb("w_plane%d_%d" % (g, t), [P, T], F32) for t in range(PACK)] for g in range(PASSES)]
+        xm_rows = xm[0].rearrange("(p t) d -> p t d", t=PACK)
+        w_planes = [[None] * PACK for g in range(PASSES)]
         x_raw = [sb("x_raw%d" % g, [P, PACK, R], F32) for g in range(PASSES)]
         v_table = sb("v_table", [P, T], U32)
-        nc.sync.dma_start(w_planes[0][0][:], w_rows[0, 0])
+        xm_raw = []
+
+        def load_plane(g, t, tag=None):
+            w_planes[g][t] = sb("w_plane%d_%d" % (g, t), [P, T], F32, tag)
+            nc.sync.dma_start(w_planes[g][t][:], w_rows[g, t])
+
+        def load_xm(count, tag):
+            first = len(xm_raw) * P
+            raw = sb("xm_raw%d" % len(xm_raw), [P, PACK, count * P], F32, tag)
+            nc.sync.dma_start(raw[:], xm_rows[:, :, first : first + count * P])
+            xm_raw.extend(raw[:, :, u * P : (u + 1) * P] for u in range(count))
+
+        load_plane(0, 0)
         nc.sync.dma_start(offsets[:], offs)
-        scale_rows = v_scales.bitcast(I32).rearrange("o (q f) t -> f q o t", f=4)
-        for f in range(4):
-            nc.sync.dma_start(
-                v_scale_table[f:P:32, :].bitcast(I32).rearrange("q (o t) -> q o t", o=PASSES), scale_rows[f]
-            )
+        nc.sync.dma_start(
+            v_scale_table[0:P:8, :].bitcast(I32).rearrange("f (o t) -> f o t", o=PASSES),
+            v_scales.bitcast(I32).rearrange("o f t -> f o t"),
+        )
         for u in range(2):
             nc.sync.dma_start(x_raw[0][:, 2 * u : 2 * u + 2, :], x_rows[0, :, 2 * u : 2 * u + 2, :])
-        nc.sync.dma_start(w_planes[0][1][:], w_rows[0, 1])
+        load_plane(0, 1)
         for u in range(2):
             nc.sync.dma_start(x_raw[1][:, 2 * u : 2 * u + 2, :], x_rows[1, :, 2 * u : 2 * u + 2, :])
         nc.sync.dma_start(v_table[:].bitcast(I32), v_words[0].rearrange("p t b -> p (t b)").bitcast(I32))
         for t in range(2, PACK):
-            nc.sync.dma_start(w_planes[0][t][:], w_rows[0, t])
-        for t in range(PACK):
-            nc.sync.dma_start(w_planes[1][t][:], w_rows[1, t])
-        xm_rows = xm[0].rearrange("(p t) d -> p t d", t=PACK)
-        xm_raw = []
-        first = 0
-        for c, width in enumerate(XM_LOADS):
-            raw = sb("xm_raw%d" % c, [P, PACK, width], F32)
-            nc.sync.dma_start(raw[:], xm_rows[:, :, first : first + width])
-            xm_raw.extend(raw[:, :, u * P : (u + 1) * P] for u in range(width // P))
-            first = first + width
+            load_plane(0, t)
 
         x_codes, x_scales = [], []
         for g in range(PASSES):
@@ -103,9 +104,18 @@ def tile_attend_gds_nce_kernel(tc, xT, wT, v_words, v_scales, wt, xm, offs, out)
             x_scales.append(sb("x_scales%d" % g, [P, R], U8))
             quantize(nc, x_codes[g][:], x_scales[g][:], grouped[:], E4M3)
 
-        v_slot_scales = sb("v_slot_scales", [P, PASSES, N], U8)
+        v_picked_scales = sb("v_picked_scales", [P, PASSES * N], U8, "x_grouped0")
         for g in range(PASSES):
-            nc.vector.tensor_copy(v_slot_scales[:, g, :], v_scale_table[:, g * T : (g + 1) * T].indirect(offsets[:]))
+            nc.vector.tensor_copy(
+                v_picked_scales[:, g * N : (g + 1) * N], v_scale_table[:, g * T : (g + 1) * T].indirect(offsets[:])
+            )
+        v_slot_rows = sb("v_slot_rows", [P, PASSES * N], U8)
+        nc.vector.memset(v_slot_rows[:].bitcast(I32), 0)
+        for f in range(4):
+            nc.sync.dma_start(v_slot_rows[f:P:32, :].bitcast(I32), v_picked_scales[8 * f : P : 32, :].bitcast(I32))
+        v_slot_scales = v_slot_rows[:].rearrange("p (o n) -> p o n", o=PASSES)
+        load_plane(1, 0, "v_scale_table")
+        load_plane(1, 1, "x_raw1")
 
         w_grouped = [[sb("w_grouped%d_%d" % (g, h), [P, HALF, PACK], BF16) for h in range(2)] for g in range(PASSES)]
 
@@ -166,13 +176,18 @@ def tile_attend_gds_nce_kernel(tc, xT, wT, v_words, v_scales, wt, xm, offs, out)
                 tanh_and_turn("teacher", q, score_banks[q], -0.5, True)
 
         teacher()
+        load_plane(1, 2, "v_table")
 
         for t in range(PACK):
             gather_plane(0, t)
+        load_plane(1, 3, "w_plane0_2")
+        load_xm(1, "w_plane0_3")
         gather_plane(1, 0)
-        for h in range(2):
+        load_xm(3, "v_scale_table")
+        for h, tag in enumerate(("x_raw1", "v_table")):
             gather_plane(1, 1 + h)
-            student_pass(0, h, "w_plane1_%d" % (1 + h))
+            student_pass(0, h, tag)
+        load_xm(4, "w_grouped0_0")
         for h in range(2):
             gather_plane(1, PACK - 1, (h,))
             student_pass(1, h, None)

@@ -49,12 +49,15 @@ def tile_attend_gds_nce_kernel(tc, xT, wT, v_words, v_scales, wt, xm, offs, out)
 
         offsets = held.tile([P, N // 16], U16, name="offsets")
         half_lists = [offsets[:, h * (HALF // 16) : (h + 1) * (HALF // 16)] for h in range(2)]
+        half_slots = [slice(h * HALF, (h + 1) * HALF) for h in range(2)]
 
         diff_banks = [psum.tile([P, R], F32, name="diff_bank%d" % q) for q in range(SLOT_TILES)]
         score_banks = [psum.tile([P, R], F32, name="score_bank%d" % q) for q in range(SLOT_TILES)]
 
         v_scale_table = sb("v_scale_table", [P, PASSES * T], U8)
         nc.vector.memset(v_scale_table[:].bitcast(I32), 0)
+        v_slot_rows = sb("v_slot_rows", [P, PASSES * N], U8)
+        nc.vector.memset(v_slot_rows[:].bitcast(I32), 0)
         windows = [sb("window%d" % i, [P, T], F32) for i in range(WINDOWS)]
         g_codes = sb("g_codes", [P, HALF + N], U32)
         g_scales = sb("g_scales", [P, HALF + N], U8)
@@ -63,17 +66,22 @@ def tile_attend_gds_nce_kernel(tc, xT, wT, v_words, v_scales, wt, xm, offs, out)
         row_weights = sb("row_weights", [P, PACK], F32)
         nc.scalar.dma_start(row_weights[:], wt[0].rearrange("(p j) o -> p (j o)", j=PACK))
 
-        w_rows = wT.rearrange("(g p t) c -> g t p c", p=P, t=PACK)
+        w_rows = wT.rearrange("(g p t) c -> g p t c", p=P, t=PACK)
         x_rows = xT[0].rearrange("(g p t) r -> g p t r", p=P, t=PACK)
         xm_rows = xm[0].rearrange("(p t) d -> p t d", t=PACK)
-        w_planes = [[None] * PACK for g in range(PASSES)]
-        x_raw = [sb("x_raw%d" % g, [P, PACK, R], F32) for g in range(PASSES)]
-        v_table = sb("v_table", [P, T], U32)
+        w_planes = {}
         xm_raw = []
 
-        def load_plane(g, t, tag=None):
-            w_planes[g][t] = sb("w_plane%d_%d" % (g, t), [P, T], F32, tag)
-            nc.sync.dma_start(w_planes[g][t][:], w_rows[g, t])
+        def load_planes(g, first, count, tag=None):
+            planes = sb("w_planes%d_%d" % (g, first), [P, count * T], F32, tag)
+            nc.sync.dma_start(planes[:], w_rows[g, :, first : first + count, :].rearrange("p t c -> p (t c)"))
+            for u in range(count):
+                w_planes[g, first + u] = planes[:, u * T : (u + 1) * T]
+
+        def load_x(g):
+            raw = sb("x_raw%d" % g, [P, PACK, R], F32)
+            nc.sync.dma_start(raw[:], x_rows[g])
+            return raw
 
         def load_xm(count, tag):
             first = len(xm_raw) * P
@@ -81,20 +89,26 @@ def tile_attend_gds_nce_kernel(tc, xT, wT, v_words, v_scales, wt, xm, offs, out)
             nc.sync.dma_start(raw[:], xm_rows[:, :, first : first + count * P])
             xm_raw.extend(raw[:, :, u * P : (u + 1) * P] for u in range(count))
 
-        load_plane(0, 0)
+        x_raw = [load_x(0)]
         nc.sync.dma_start(offsets[:], offs)
         nc.sync.dma_start(
             v_scale_table[0:P:8, :].bitcast(I32).rearrange("f (o t) -> f o t", o=PASSES),
             v_scales.bitcast(I32).rearrange("o f t -> f o t"),
         )
-        for u in range(2):
-            nc.sync.dma_start(x_raw[0][:, 2 * u : 2 * u + 2, :], x_rows[0, :, 2 * u : 2 * u + 2, :])
-        load_plane(0, 1)
-        for u in range(2):
-            nc.sync.dma_start(x_raw[1][:, 2 * u : 2 * u + 2, :], x_rows[1, :, 2 * u : 2 * u + 2, :])
+        load_planes(0, 0, 2)
+        x_raw.append(load_x(1))
+        v_table = sb("v_table", [P, T], U32)
         nc.sync.dma_start(v_table[:].bitcast(I32), v_words[0].rearrange("p t b -> p (t b)").bitcast(I32))
-        for t in range(2, PACK):
-            load_plane(0, t)
+
+        v_picked_scales = sb("v_picked_scales", [P, PASSES * N], U8)
+        for g in range(PASSES):
+            nc.vector.tensor_copy(
+                v_picked_scales[:, g * N : (g + 1) * N], v_scale_table[:, g * T : (g + 1) * T].indirect(offsets[:])
+            )
+        for f in range(4):
+            nc.sync.dma_start(v_slot_rows[f:P:32, :].bitcast(I32), v_picked_scales[8 * f : P : 32, :].bitcast(I32))
+        v_slot_scales = v_slot_rows[:].rearrange("p (o n) -> p o n", o=PASSES)
+        load_planes(0, 2, 2, "v_scale_table")
 
         x_codes, x_scales = [], []
         for g in range(PASSES):
@@ -104,24 +118,14 @@ def tile_attend_gds_nce_kernel(tc, xT, wT, v_words, v_scales, wt, xm, offs, out)
             x_scales.append(sb("x_scales%d" % g, [P, R], U8))
             quantize(nc, x_codes[g][:], x_scales[g][:], grouped[:], E4M3)
 
-        v_picked_scales = sb("v_picked_scales", [P, PASSES * N], U8, "x_grouped0")
-        for g in range(PASSES):
-            nc.vector.tensor_copy(
-                v_picked_scales[:, g * N : (g + 1) * N], v_scale_table[:, g * T : (g + 1) * T].indirect(offsets[:])
-            )
-        v_slot_rows = sb("v_slot_rows", [P, PASSES * N], U8)
-        nc.vector.memset(v_slot_rows[:].bitcast(I32), 0)
-        for f in range(4):
-            nc.sync.dma_start(v_slot_rows[f:P:32, :].bitcast(I32), v_picked_scales[8 * f : P : 32, :].bitcast(I32))
-        v_slot_scales = v_slot_rows[:].rearrange("p (o n) -> p o n", o=PASSES)
-        load_plane(1, 0, "v_scale_table")
-        load_plane(1, 1, "x_raw1")
-
         w_grouped = [[sb("w_grouped%d_%d" % (g, h), [P, HALF, PACK], BF16) for h in range(2)] for g in range(PASSES)]
+        w_picked = [sb("w_picked0", [P, PACK, N], F32), sb("w_picked1", [P, 2, N], F32)]
 
-        def gather_plane(g, t, halves=(0, 1)):
-            for h in halves:
-                nc.vector.tensor_copy(w_grouped[g][h][:, :, t], w_planes[g][t][:].indirect(half_lists[h]))
+        def pick_plane(g, t):
+            nc.vector.tensor_copy(w_picked[g][:, t, :], w_planes[g, t].indirect(offsets[:]))
+
+        def pick_in_place(t, h):
+            nc.vector.tensor_copy(w_grouped[1][h][:, :, t], w_planes[1, t].indirect(half_lists[h]))
 
         def student_pass(g, h, tag):
             codes = sb("w_codes%d_%d" % (g, h), [P, HALF], U32, tag)
@@ -175,30 +179,40 @@ def tile_attend_gds_nce_kernel(tc, xT, wT, v_words, v_scales, wt, xm, offs, out)
             for q in range(SLOT_TILES):
                 tanh_and_turn("teacher", q, score_banks[q], -0.5, True)
 
+        for t in range(2):
+            pick_plane(0, t)
+        load_planes(1, 0, 1, "w_planes0_0")
         teacher()
-        load_plane(1, 2, "v_table")
-
-        for t in range(PACK):
-            gather_plane(0, t)
-        load_plane(1, 3, "w_plane0_2")
-        load_xm(1, "w_plane0_3")
-        gather_plane(1, 0)
-        load_xm(3, "v_scale_table")
-        for h, tag in enumerate(("x_raw1", "v_table")):
-            gather_plane(1, 1 + h)
-            student_pass(0, h, tag)
-        load_xm(4, "w_grouped0_0")
+        load_planes(1, 1, 1, "v_table")
+        load_planes(1, 2, 1, "x_grouped1")
+        for t in range(2, PACK):
+            pick_plane(0, t)
+        load_planes(1, 3, 1, "v_scale_table")
         for h in range(2):
-            gather_plane(1, PACK - 1, (h,))
+            interleave(nc, w_grouped[0][h][:], w_picked[0][:, :, half_slots[h]])
+        pick_plane(1, 0)
+        load_xm(1, "w_planes0_0")
+        pick_plane(1, 1)
+        for h in range(2):
+            interleave(nc, w_grouped[1][h][:, :, 0:2], w_picked[1][:, :, half_slots[h]])
+        student_pass(0, 0, "v_table")
+        load_xm(3, "w_grouped0_0")
+        for h in range(2):
+            pick_in_place(2, h)
+        student_pass(0, 1, "x_grouped1")
+        load_xm(4, "w_grouped0_1")
+
+        for h in range(2):
+            pick_in_place(PACK - 1, h)
             student_pass(1, h, None)
 
         xm_codes, xm_scales = [], []
 
-        def quantize_xm(first, count, tag):
+        def quantize_xm(first, count, tag, codes_tag=None):
             grouped = sb("xm_grouped%d" % first, [P, count * P, PACK], BF16, tag)
             for u in range(count):
                 interleave(nc, grouped[:, u * P : (u + 1) * P, :], xm_raw[first + u])
-            codes = sb("xm_codes%d" % first, [P, count * P], U32)
+            codes = sb("xm_codes%d" % first, [P, count * P], U32, codes_tag)
             scales = sb("xm_scales%d" % first, [P, count * P], U8)
             quantize(nc, codes[:], scales[:], grouped[:], E4M3)
             for u in range(count):
@@ -216,7 +230,7 @@ def tile_attend_gds_nce_kernel(tc, xT, wT, v_words, v_scales, wt, xm, offs, out)
                 stop=True,
             )
 
-        quantize_xm(0, 1, None)
+        quantize_xm(0, 1, "w_picked1", "w_grouped1_0")
 
         half_weights = sb("half_weights", [P, P, PACK], F32)
         nc.vector.tensor_scalar_mul(half_weights[:], row_weights[:].unsqueeze(1).to_broadcast([P, P, PACK]), 0.5)

@@ -16,6 +16,7 @@ E4M3 = mybir.dt.float8_e4m3fn_x4
 E5M2 = mybir.dt.float8_e5m2_x4
 E2M1 = mybir.dt.float4_e2m1fn_x4
 TANH = mybir.ActivationFunctionType.Tanh
+COPY = mybir.ActivationFunctionType.Copy
 MULT = mybir.AluOpType.mult
 
 P = 128
@@ -25,10 +26,11 @@ PASSES = D // K_PASS
 HALF = N // 2
 SLOT_TILES = N // P
 WINDOWS = 3
+LAST_PIECES = 4
 
 
-def interleave(nc, grouped, raw):
-    nc.scalar.copy(
+def interleave(copy, grouped, raw):
+    copy(
         out=grouped.rearrange("p (c i) t -> p c t i", i=PACK),
         in_=raw.rearrange("p t (c i) -> p c t i", i=PACK),
     )
@@ -57,14 +59,11 @@ def tile_attend_gds_nce_kernel(tc, xT, wT, v_words, v_scales, wt, xm, offs, out)
         v_scale_table = sb("v_scale_table", [P, PASSES * T], U8)
         nc.vector.memset(v_scale_table[:].bitcast(I32), 0)
         v_slot_rows = sb("v_slot_rows", [P, PASSES * N], U8)
-        nc.vector.memset(v_slot_rows[:].bitcast(I32), 0)
         windows = [sb("window%d" % i, [P, T], F32) for i in range(WINDOWS)]
         g_codes = sb("g_codes", [P, HALF + N], U32)
         g_scales = sb("g_scales", [P, HALF + N], U8)
         identity = sb("identity", [P, P], F32)
         make_identity(nc, identity[:])
-        row_weights = sb("row_weights", [P, PACK], F32)
-        nc.scalar.dma_start(row_weights[:], wt[0].rearrange("(p j) o -> p (j o)", j=PACK))
 
         w_rows = wT.rearrange("(g p t) c -> g p t c", p=P, t=PACK)
         x_rows = xT[0].rearrange("(g p t) r -> g p t r", p=P, t=PACK)
@@ -105,7 +104,8 @@ def tile_attend_gds_nce_kernel(tc, xT, wT, v_words, v_scales, wt, xm, offs, out)
             nc.vector.tensor_copy(
                 v_picked_scales[:, g * N : (g + 1) * N], v_scale_table[:, g * T : (g + 1) * T].indirect(offsets[:])
             )
-        for f in range(4):
+        nc.vector.tensor_copy(v_slot_rows[:].bitcast(I32), v_picked_scales[:].bitcast(I32))
+        for f in range(1, 4):
             nc.sync.dma_start(v_slot_rows[f:P:32, :].bitcast(I32), v_picked_scales[8 * f : P : 32, :].bitcast(I32))
         v_slot_scales = v_slot_rows[:].rearrange("p (o n) -> p o n", o=PASSES)
         load_planes(0, 2, 2, "v_scale_table")
@@ -113,16 +113,16 @@ def tile_attend_gds_nce_kernel(tc, xT, wT, v_words, v_scales, wt, xm, offs, out)
         x_codes, x_scales = [], []
         for g in range(PASSES):
             grouped = sb("x_grouped%d" % g, [P, R, PACK], BF16)
-            interleave(nc, grouped[:], x_raw[g][:])
+            interleave(nc.scalar.copy, grouped[:], x_raw[g][:])
             x_codes.append(sb("x_codes%d" % g, [P, R], U32))
             x_scales.append(sb("x_scales%d" % g, [P, R], U8))
             quantize(nc, x_codes[g][:], x_scales[g][:], grouped[:], E4M3)
 
         w_grouped = [[sb("w_grouped%d_%d" % (g, h), [P, HALF, PACK], BF16) for h in range(2)] for g in range(PASSES)]
-        w_picked = [sb("w_picked0", [P, PACK, N], F32), sb("w_picked1", [P, 2, N], F32)]
+        w_picked = sb("w_picked", [P, PACK, N], F32)
 
-        def pick_plane(g, t):
-            nc.vector.tensor_copy(w_picked[g][:, t, :], w_planes[g, t].indirect(offsets[:]))
+        def pick_plane(t):
+            nc.vector.tensor_copy(w_picked[:, t, :], w_planes[0, t].indirect(offsets[:]))
 
         def pick_in_place(t, h):
             nc.vector.tensor_copy(w_grouped[1][h][:, :, t], w_planes[1, t].indirect(half_lists[h]))
@@ -180,39 +180,51 @@ def tile_attend_gds_nce_kernel(tc, xT, wT, v_words, v_scales, wt, xm, offs, out)
                 tanh_and_turn("teacher", q, score_banks[q], -0.5, True)
 
         for t in range(2):
-            pick_plane(0, t)
-        load_planes(1, 0, 1, "w_planes0_0")
+            pick_plane(t)
+        load_planes(1, 2, 1, "w_planes0_0")
         teacher()
-        load_planes(1, 1, 1, "v_table")
-        load_planes(1, 2, 1, "x_grouped1")
+        load_planes(1, 0, 1, "v_table")
+        load_planes(1, 1, 1, "x_grouped1")
         for t in range(2, PACK):
-            pick_plane(0, t)
-        load_planes(1, 3, 1, "v_scale_table")
+            pick_plane(t)
+        last_plane = sb("last_plane", [P, T], F32, "v_scale_table")
+        pieces = [slice(u * T // LAST_PIECES, (u + 1) * T // LAST_PIECES) for u in range(LAST_PIECES)]
+        for cols in pieces:
+            nc.sync.dma_start(last_plane[:, cols], w_rows[1, :, PACK - 1, cols])
+        w_planes[1, PACK - 1] = last_plane[:]
         for h in range(2):
-            interleave(nc, w_grouped[0][h][:], w_picked[0][:, :, half_slots[h]])
-        pick_plane(1, 0)
-        load_xm(1, "w_planes0_0")
-        pick_plane(1, 1)
+            interleave(nc.scalar.copy, w_grouped[0][h][:], w_picked[:, :, half_slots[h]])
+        pick_in_place(2, 0)
+        third_picked = sb("third_picked", [P, HALF], F32)
+        nc.vector.tensor_copy(third_picked[:], w_planes[1, 2].indirect(half_lists[1]))
+        nc.scalar.copy(out=w_grouped[1][1][:, :, 2], in_=third_picked[:])
+        row_weights = sb("row_weights", [P, PACK], F32, "w_planes0_0")
+        nc.sync.dma_start(row_weights[:], wt[0].rearrange("(p j) o -> p (j o)", j=PACK))
+        load_xm(2, "w_picked")
         for h in range(2):
-            interleave(nc, w_grouped[1][h][:, :, 0:2], w_picked[1][:, :, half_slots[h]])
+            pick_in_place(0, h)
         student_pass(0, 0, "v_table")
-        load_xm(3, "w_grouped0_0")
+        load_xm(2, "w_grouped0_0")
         for h in range(2):
-            pick_in_place(2, h)
+            pick_in_place(1, h)
         student_pass(0, 1, "x_grouped1")
         load_xm(4, "w_grouped0_1")
 
-        for h in range(2):
-            pick_in_place(PACK - 1, h)
-            student_pass(1, h, None)
+        last_rounded = sb("last_rounded", [P, T], BF16)
+        for cols in pieces:
+            nc.scalar.activation(last_rounded[:, cols], last_plane[:, cols], COPY)
+        pick_in_place(PACK - 1, 0)
+        student_pass(1, 0, None)
+        nc.scalar.activation(w_grouped[1][1][:, :, PACK - 1], last_rounded[:].indirect(half_lists[1]), COPY)
+        student_pass(1, 1, None)
 
         xm_codes, xm_scales = [], []
 
-        def quantize_xm(first, count, tag, codes_tag=None):
+        def quantize_xm(first, count, tag, copy=nc.scalar.copy):
             grouped = sb("xm_grouped%d" % first, [P, count * P, PACK], BF16, tag)
             for u in range(count):
-                interleave(nc, grouped[:, u * P : (u + 1) * P, :], xm_raw[first + u])
-            codes = sb("xm_codes%d" % first, [P, count * P], U32, codes_tag)
+                interleave(copy, grouped[:, u * P : (u + 1) * P, :], xm_raw[first + u])
+            codes = sb("xm_codes%d" % first, [P, count * P], U32)
             scales = sb("xm_scales%d" % first, [P, count * P], U8)
             quantize(nc, codes[:], scales[:], grouped[:], E4M3)
             for u in range(count):
@@ -230,16 +242,19 @@ def tile_attend_gds_nce_kernel(tc, xT, wT, v_words, v_scales, wt, xm, offs, out)
                 stop=True,
             )
 
-        quantize_xm(0, 1, "w_picked1", "w_grouped1_0")
+        quantize_xm(0, 2, "w_grouped1_1", nc.vector.tensor_copy)
 
-        half_weights = sb("half_weights", [P, P, PACK], F32)
-        nc.vector.tensor_scalar_mul(half_weights[:], row_weights[:].unsqueeze(1).to_broadcast([P, P, PACK]), 0.5)
         first_dw = [sb("first_dw%d" % h, [P, HALF], F32) for h in range(2)]
         for q in range(SLOT_TILES):
             tanh_and_turn("student", q, score_banks[q], 0.5, False)
             g_grouped = sb("g_grouped%d" % q, [P, P, PACK], BF16)
-            nc.vector.tensor_tensor(
-                g_grouped[:], diff_banks[q][:].rearrange("p (j n) -> p n j", j=PACK), half_weights[:], MULT
+            nc.vector.scalar_tensor_tensor(
+                g_grouped[:],
+                diff_banks[q][:].rearrange("p (j n) -> p n j", j=PACK),
+                0.5,
+                row_weights[:].unsqueeze(1).to_broadcast([P, P, PACK]),
+                MULT,
+                MULT,
             )
             cols = slice(HALF + q * P, HALF + (q + 1) * P)
             quantize(nc, g_codes[:, cols], g_scales[:, cols], g_grouped[:], E5M2)
@@ -265,8 +280,7 @@ def tile_attend_gds_nce_kernel(tc, xT, wT, v_words, v_scales, wt, xm, offs, out)
             nc.vector.tensor_copy(window[:].indirect(offsets[:]), dw[:])
             nc.sync.dma_start(out[m * P : (m + 1) * P, :], window[:])
 
-        quantize_xm(1, 1, "student_tanh0")
-        quantize_xm(2, 2, "student_tanh1")
+        quantize_xm(2, 2, "student_tanh2")
         finish(1)
         quantize_xm(4, 4, "g_grouped%d" % (SLOT_TILES - 1))
         for m in range(2, D // P):

@@ -27,6 +27,7 @@ HALF = N // 2
 SLOT_TILES = N // P
 WINDOWS = 3
 LAST_PIECES = 4
+LOAD_TAGS = ("v_scale_table", "w_planes0_0", "v_table", "x_grouped1", "x_raw0", "x_raw1", "w_picked")
 
 
 def interleave(copy, grouped, raw):
@@ -43,11 +44,16 @@ def quantize(nc, codes, scales, grouped, fmt):
 def tile_attend_gds_nce_kernel(tc, xT, wT, v_words, v_scales, wt, xm, offs, out):
     nc = tc.nc
     with ExitStack() as ctx:
+        low = ctx.enter_context(tc.tile_pool(name="low", bufs=1))
+        loads = ctx.enter_context(tc.tile_pool(name="loads", bufs=1))
+        middle = ctx.enter_context(tc.tile_pool(name="middle", bufs=1))
         held = ctx.enter_context(tc.tile_pool(name="held", bufs=1))
+        high = ctx.enter_context(tc.tile_pool(name="high", bufs=1))
         psum = ctx.enter_context(tc.psum_pool(name="psum", bufs=1))
 
         def sb(name, shape, dtype, tag=None):
-            return held.tile(shape, dtype, name=name, tag=tag or name, align_bytes=64)
+            pool = loads if (tag or name) in LOAD_TAGS else held
+            return pool.tile(shape, dtype, name=name, tag=tag or name, align_bytes=64)
 
         offsets = held.tile([P, N // 16], U16, name="offsets")
         half_lists = [offsets[:, h * (HALF // 16) : (h + 1) * (HALF // 16)] for h in range(2)]
@@ -59,7 +65,7 @@ def tile_attend_gds_nce_kernel(tc, xT, wT, v_words, v_scales, wt, xm, offs, out)
         v_scale_table = sb("v_scale_table", [P, PASSES * T], U8)
         nc.vector.memset(v_scale_table[:].bitcast(I32), 0)
         v_slot_rows = sb("v_slot_rows", [P, PASSES * N], U8)
-        windows = [sb("window%d" % i, [P, T], F32) for i in range(WINDOWS)]
+        windows = [pool.tile([P, T], F32, name="window%d" % i) for i, pool in enumerate((low, middle, high))]
         g_codes = sb("g_codes", [P, HALF + N], U32)
         g_scales = sb("g_scales", [P, HALF + N], U8)
         identity = sb("identity", [P, P], F32)
@@ -130,9 +136,12 @@ def tile_attend_gds_nce_kernel(tc, xT, wT, v_words, v_scales, wt, xm, offs, out)
         def student_pass(g, h, tag):
             codes = sb("w_codes%d_%d" % (g, h), [P, HALF], U32, tag)
             scales = sb("w_scales%d_%d" % (g, h), [P, HALF], U8)
-            quantize(nc, codes[:], scales[:], w_grouped[g][h][:], E4M3)
+            if g == 0:
+                quantize(nc, codes[:], scales[:], w_grouped[g][h][:], E4M3)
             for u in range(2):
                 cols = slice(u * P, (u + 1) * P)
+                if g == 1:
+                    quantize(nc, codes[:, cols], scales[:, cols], w_grouped[g][h][:, cols, :], E4M3)
                 nc.tensor.matmul_mx(
                     out=score_banks[2 * h + u][:],
                     lhsT=codes[:, cols].bitcast(E4M3),

@@ -119,7 +119,10 @@ def tile_attend_gds_nce_kernel(tc, xT, wT, v_words, v_scales, wt, xm, offs, out)
         x_codes, x_scales = [], []
         for g in range(PASSES):
             grouped = sb("x_grouped%d" % g, [P, R, PACK], BF16)
-            interleave(nc.scalar.copy, grouped[:], x_raw[g][:])
+            nc.scalar.copy(
+                out=grouped[:].rearrange("p (j s) t -> p s t j", j=PACK),
+                in_=x_raw[g][:].rearrange("p t (s j) -> p s t j", j=PACK),
+            )
             x_codes.append(sb("x_codes%d" % g, [P, R], U32))
             x_scales.append(sb("x_scales%d" % g, [P, R], U8))
             quantize(nc, x_codes[g][:], x_scales[g][:], grouped[:], E4M3)
@@ -154,7 +157,7 @@ def tile_attend_gds_nce_kernel(tc, xT, wT, v_words, v_scales, wt, xm, offs, out)
 
         def tanh_and_turn(name, q, scores, scale, opens):
             halves = sb("%s_tanh%d" % (name, q), [P, PACK, P], F32)
-            nc.scalar.activation(halves[:], scores[:].rearrange("p (s j) -> p j s", j=PACK), TANH, scale=scale)
+            nc.scalar.activation(halves[:], scores[:].rearrange("p (j s) -> p j s", j=PACK), TANH, scale=scale)
             for j in range(PACK):
                 nc.tensor.matmul(
                     diff_banks[q][:, j * P : (j + 1) * P],

@@ -256,16 +256,16 @@ def tile_attend_gds_nce_kernel(tc, xT, wT, v_words, v_scales, wt, xm, offs, out)
 
         quantize_xm(0, 2, "w_grouped1_1", nc.vector.tensor_copy)
 
+        half_weights = sb("half_weights", [P, PACK], F32, "w_grouped1_0")
+        nc.vector.tensor_scalar_mul(half_weights[:], row_weights[:], 0.5)
         first_dw = [sb("first_dw%d" % h, [P, HALF], F32) for h in range(2)]
         for q in range(SLOT_TILES):
             tanh_and_turn("student", q, score_banks[q], 0.5, False)
             g_grouped = sb("g_grouped%d" % q, [P, P, PACK], BF16)
-            nc.vector.scalar_tensor_tensor(
-                g_grouped[:],
-                diff_banks[q][:].rearrange("p (j n) -> p n j", j=PACK),
-                0.5,
-                row_weights[:].unsqueeze(1).to_broadcast([P, P, PACK]),
-                MULT,
+            nc.vector.tensor_tensor(
+                g_grouped[:].rearrange("p (c i) j -> p c j i", i=PACK),
+                diff_banks[q][:].rearrange("p (j c i) -> p c j i", j=PACK, i=PACK),
+                half_weights[:].unsqueeze(1).unsqueeze(3).to_broadcast([P, P // PACK, PACK, PACK]),
                 MULT,
             )
             cols = slice(HALF + q * P, HALF + (q + 1) * P)

@@ -210,11 +210,11 @@ def tile_attend_gds_nce_kernel(tc, xT, wT, v_words, v_scales, wt, xm, offs, out)
         third_picked = sb("third_picked", [P, HALF], F32)
         nc.vector.tensor_copy(third_picked[:], w_planes[1, 2].indirect(half_lists[1]))
         nc.scalar.copy(out=w_grouped[1][1][:, :, 2], in_=third_picked[:])
-        row_weights = sb("row_weights", [P, PACK], F32, "w_planes0_0")
-        nc.sync.dma_start(row_weights[:], wt[0].rearrange("(p j) o -> p (j o)", j=PACK))
         load_xm(2, "w_picked")
         for h in range(2):
             pick_in_place(0, h)
+        row_weights = sb("row_weights", [P, PACK], F32, "third_picked")
+        nc.sync.dma_start(row_weights[:], wt[0].rearrange("(p j) o -> p (j o)", j=PACK))
         student_pass(0, 0, "v_table")
         load_xm(2, "w_grouped0_0")
         for h in range(2):
@@ -256,16 +256,16 @@ def tile_attend_gds_nce_kernel(tc, xT, wT, v_words, v_scales, wt, xm, offs, out)
 
         quantize_xm(0, 2, "w_grouped1_1", nc.vector.tensor_copy)
 
-        half_weights = sb("half_weights", [P, PACK], F32, "w_grouped1_0")
-        nc.vector.tensor_scalar_mul(half_weights[:], row_weights[:], 0.5)
         first_dw = [sb("first_dw%d" % h, [P, HALF], F32) for h in range(2)]
         for q in range(SLOT_TILES):
             tanh_and_turn("student", q, score_banks[q], 0.5, False)
             g_grouped = sb("g_grouped%d" % q, [P, P, PACK], BF16)
-            nc.vector.tensor_tensor(
-                g_grouped[:].rearrange("p (c i) j -> p c j i", i=PACK),
-                diff_banks[q][:].rearrange("p (j c i) -> p c j i", j=PACK, i=PACK),
-                half_weights[:].unsqueeze(1).unsqueeze(3).to_broadcast([P, P // PACK, PACK, PACK]),
+            nc.vector.scalar_tensor_tensor(
+                g_grouped[:],
+                diff_banks[q][:].rearrange("p (j s) -> p s j", j=PACK),
+                0.5,
+                row_weights[:].unsqueeze(1).to_broadcast([P, P, PACK]),
+                MULT,
                 MULT,
             )
             cols = slice(HALF + q * P, HALF + (q + 1) * P)

@@ -25,7 +25,8 @@ K_PASS = P * PACK
 PASSES = D // K_PASS
 HALF = N // 2
 SLOT_TILES = N // P
-WINDOWS = 3
+WINDOWS = 4
+KIB = 1024
 LAST_PIECES = 4
 LOAD_TAGS = ("v_scale_table", "w_planes0_0", "v_table", "x_grouped1", "x_raw0", "x_raw1", "w_picked")
 
@@ -49,11 +50,15 @@ def tile_attend_gds_nce_kernel(tc, xT, wT, v_words, v_scales, wt, xm, offs, out)
         middle = ctx.enter_context(tc.tile_pool(name="middle", bufs=1))
         held = ctx.enter_context(tc.tile_pool(name="held", bufs=1))
         high = ctx.enter_context(tc.tile_pool(name="high", bufs=1))
+        stage = ctx.enter_context(tc.tile_pool(name="stage", bufs=1))
         psum = ctx.enter_context(tc.psum_pool(name="psum", bufs=1))
 
         def sb(name, shape, dtype, tag=None):
             pool = loads if (tag or name) in LOAD_TAGS else held
             return pool.tile(shape, dtype, name=name, tag=tag or name, align_bytes=64)
+
+        def staged(name, shape, dtype, at):
+            return stage.tile(shape, dtype, name=name, align_bytes=64, offset=at)
 
         offsets = held.tile([P, N // 16], U16, name="offsets")
         half_lists = [offsets[:, h * (HALF // 16) : (h + 1) * (HALF // 16)] for h in range(2)]
@@ -66,8 +71,8 @@ def tile_attend_gds_nce_kernel(tc, xT, wT, v_words, v_scales, wt, xm, offs, out)
         nc.vector.memset(v_scale_table[:].bitcast(I32), 0)
         v_slot_rows = sb("v_slot_rows", [P, PASSES * N], U8)
         windows = [pool.tile([P, T], F32, name="window%d" % i) for i, pool in enumerate((low, middle, high))]
-        g_codes = sb("g_codes", [P, HALF + N], U32)
-        g_scales = sb("g_scales", [P, HALF + N], U8)
+        g_codes = sb("g_codes", [P, N], U32)
+        g_scales = sb("g_scales", [P, N], U8)
         identity = sb("identity", [P, P], F32)
         make_identity(nc, identity[:])
 
@@ -131,7 +136,10 @@ def tile_attend_gds_nce_kernel(tc, xT, wT, v_words, v_scales, wt, xm, offs, out)
         w_picked = sb("w_picked", [P, PACK, N], F32)
 
         def pick_plane(t):
-            nc.vector.tensor_copy(w_picked[:, t, :], w_planes[0, t].indirect(offsets[:]))
+            if t < 2:
+                nc.scalar.activation(w_picked[:, t, :], w_planes[0, t].indirect(offsets[:]), COPY)
+            else:
+                nc.vector.tensor_copy(w_picked[:, t, :], w_planes[0, t].indirect(offsets[:]))
 
         def pick_in_place(t, h):
             nc.vector.tensor_copy(w_grouped[1][h][:, :, t], w_planes[1, t].indirect(half_lists[h]))
@@ -230,36 +238,44 @@ def tile_attend_gds_nce_kernel(tc, xT, wT, v_words, v_scales, wt, xm, offs, out)
         nc.scalar.activation(w_grouped[1][1][:, :, PACK - 1], last_rounded[:].indirect(half_lists[1]), COPY)
         student_pass(1, 1, None)
 
-        xm_codes, xm_scales = [], []
+        xm_codes, xm_scales = {}, {}
 
-        def quantize_xm(first, count, tag, copy=nc.scalar.copy):
-            grouped = sb("xm_grouped%d" % first, [P, count * P, PACK], BF16, tag)
+        def lay_out_xm(first, count, grouped, copy):
             for u in range(count):
                 interleave(copy, grouped[:, u * P : (u + 1) * P, :], xm_raw[first + u])
+
+        def quantize_xm(first, count, grouped, scales=None):
             codes = sb("xm_codes%d" % first, [P, count * P], U32)
-            scales = sb("xm_scales%d" % first, [P, count * P], U8)
+            if scales is None:
+                scales = sb("xm_scales%d" % first, [P, count * P], U8)
             quantize(nc, codes[:], scales[:], grouped[:], E4M3)
             for u in range(count):
-                xm_codes.append(codes[:, u * P : (u + 1) * P])
-                xm_scales.append(scales[:, u * P : (u + 1) * P])
+                xm_codes[first + u] = codes[:, u * P : (u + 1) * P]
+                xm_scales[first + u] = scales[:, u * P : (u + 1) * P]
 
-        def gradient_product(m, bank, first):
+        def gradient_product(m, bank, slots):
             nc.tensor.matmul_mx(
-                out=bank[:],
+                out=bank,
                 lhsT=xm_codes[m].bitcast(E4M3),
                 lhsT_scale=xm_scales[m],
-                rhs=g_codes[:, first : first + N].bitcast(E5M2),
-                rhs_scale=g_scales[:, first : first + N],
+                rhs=g_codes[:, slots].bitcast(E5M2),
+                rhs_scale=g_scales[:, slots],
                 start=True,
                 stop=True,
             )
 
-        quantize_xm(0, 2, "w_grouped1_1", nc.vector.tensor_copy)
+        even_area, odd_area, last_g_area = 0, 3 * KIB, 7 * KIB
 
-        first_dw = [sb("first_dw%d" % h, [P, HALF], F32) for h in range(2)]
+        grouped = sb("xm_grouped0", [P, 2 * P, PACK], BF16, "w_grouped1_1")
+        lay_out_xm(0, 2, grouped, nc.vector.tensor_copy)
+        quantize_xm(0, 2, grouped)
+
         for q in range(SLOT_TILES):
             tanh_and_turn("student", q, score_banks[q], 0.5, False)
-            g_grouped = sb("g_grouped%d" % q, [P, P, PACK], BF16)
+            if q < SLOT_TILES - 1:
+                g_grouped = sb("g_grouped%d" % q, [P, P, PACK], BF16)
+            else:
+                g_grouped = staged("g_grouped%d" % q, [P, P, PACK], BF16, last_g_area)
             nc.vector.scalar_tensor_tensor(
                 g_grouped[:],
                 diff_banks[q][:].rearrange("p (j s) -> p s j", j=PACK),
@@ -268,32 +284,59 @@ def tile_attend_gds_nce_kernel(tc, xT, wT, v_words, v_scales, wt, xm, offs, out)
                 MULT,
                 MULT,
             )
-            cols = slice(HALF + q * P, HALF + (q + 1) * P)
+            cols = slice(q * P, (q + 1) * P)
             quantize(nc, g_codes[:, cols], g_scales[:, cols], g_grouped[:], E5M2)
 
-        nc.vector.memset(g_codes[:, :HALF].bitcast(I32), 0)
-        nc.vector.memset(g_scales[:, :HALF].bitcast(I32), 0)
+        windows.append(sb("window3", [P, T], F32, "x_raw0"))
         for window in windows:
             nc.vector.memset(window[:], 0.0)
-        gradient_product(0, score_banks[0], 0)
-        nc.scalar.copy(out=first_dw[0][:], in_=score_banks[0][:, HALF:])
-        gradient_product(0, score_banks[1], HALF)
-        nc.scalar.copy(out=first_dw[1][:], in_=score_banks[1][:, HALF:])
-        for h in range(2):
-            nc.vector.tensor_copy(windows[0][:].indirect(half_lists[h]), first_dw[h][:])
-        nc.sync.dma_start(out[0:P, :], windows[0][:])
+
+        def result_tile(m):
+            area = odd_area if m % 2 else even_area
+            return staged("dw%d" % m, [P, N], F32, area + (m // 2 % 2) * KIB)
+
+        def scatter_and_store(m, dw):
+            window = windows[m % WINDOWS]
+            if m % 2:
+                nc.vector.tensor_copy(window[:].indirect(offsets[:]), dw[:])
+            else:
+                for h in range(2):
+                    nc.scalar.activation(window[:].indirect(half_lists[h]), dw[:, half_slots[h]], COPY)
+            nc.sync.dma_start(out[m * P : (m + 1) * P, :], window[:])
 
         def finish(m):
             bank = score_banks[(m + 1) % SLOT_TILES]
-            gradient_product(m, bank, HALF)
-            dw = sb("dw%d" % m, [P, N], F32)
-            nc.scalar.copy(out=dw[:], in_=bank[:])
-            window = windows[m % WINDOWS]
-            nc.vector.tensor_copy(window[:].indirect(offsets[:]), dw[:])
-            nc.sync.dma_start(out[m * P : (m + 1) * P, :], window[:])
+            gradient_product(m, bank[:], slice(0, N))
+            dw = result_tile(m)
+            copy = nc.vector.tensor_copy if m % 2 else nc.scalar.copy
+            copy(out=dw[:], in_=bank[:])
+            scatter_and_store(m, dw)
 
-        quantize_xm(2, 2, "student_tanh2")
+        dw = result_tile(0)
+        for h, copy in enumerate((nc.scalar.copy, nc.vector.tensor_copy)):
+            gradient_product(0, score_banks[h][:, :HALF], half_slots[h])
+            copy(out=dw[:, half_slots[h]], in_=score_banks[h][:, :HALF])
+        scatter_and_store(0, dw)
+
+        grouped = sb("xm_grouped2", [P, 2 * P, PACK], BF16, "student_tanh2")
+        lay_out_xm(2, 2, grouped, nc.scalar.copy)
+        quantize_xm(2, 2, grouped, staged("xm_scales2", [P, 2 * P], U8, last_g_area))
+        grouped = staged("xm_grouped4", [P, P, PACK], BF16, last_g_area + 2 * P)
+        lay_out_xm(4, 1, grouped, nc.vector.tensor_copy)
         finish(1)
-        quantize_xm(4, 4, "g_grouped%d" % (SLOT_TILES - 1))
-        for m in range(2, D // P):
-            finish(m)
+        quantize_xm(4, 1, grouped)
+        finish(2)
+        grouped = staged("xm_grouped5", [P, P, PACK], BF16, odd_area)
+        lay_out_xm(5, 1, grouped, nc.vector.tensor_copy)
+        finish(3)
+        quantize_xm(5, 1, grouped)
+        grouped = staged("xm_grouped6", [P, P, PACK], BF16, even_area + 2 * KIB)
+        lay_out_xm(6, 1, grouped, nc.scalar.copy)
+        finish(4)
+        quantize_xm(6, 1, grouped, staged("xm_scales6", [P, P], U8, odd_area + 2 * KIB))
+        grouped = staged("xm_grouped7", [P, P, PACK], BF16, odd_area + 2 * KIB + P)
+        lay_out_xm(7, 1, grouped, nc.vector.tensor_copy)
+        finish(5)
+        quantize_xm(7, 1, grouped)
+        finish(6)
+        finish(7)

@@ -27,7 +27,6 @@ HALF = N // 2
 SLOT_TILES = N // P
 WINDOWS = 4
 KIB = 1024
-LAST_PIECES = 4
 LOAD_TAGS = ("v_scale_table", "w_planes0_0", "v_table", "x_grouped1", "x_raw0", "x_raw1", "w_picked")
 
 
@@ -97,7 +96,7 @@ def tile_attend_gds_nce_kernel(tc, xT, wT, v_words, v_scales, wt, xm, offs, out)
             first = len(xm_raw) * P
             raw = sb("xm_raw%d" % len(xm_raw), [P, PACK, count * P], F32, tag)
             nc.sync.dma_start(raw[:], xm_rows[:, :, first : first + count * P])
-            xm_raw.extend(raw[:, :, u * P : (u + 1) * P] for u in range(count))
+            xm_raw.extend((raw, u * P) for u in range(count))
 
         x_raw = [load_x(0)]
         nc.sync.dma_start(offsets[:], offs)
@@ -207,21 +206,16 @@ def tile_attend_gds_nce_kernel(tc, xT, wT, v_words, v_scales, wt, xm, offs, out)
         load_planes(1, 1, 1, "x_grouped1")
         for t in range(2, PACK):
             pick_plane(t)
-        last_plane = sb("last_plane", [P, T], F32, "v_scale_table")
-        pieces = [slice(u * T // LAST_PIECES, (u + 1) * T // LAST_PIECES) for u in range(LAST_PIECES)]
-        for cols in pieces:
-            nc.sync.dma_start(last_plane[:, cols], w_rows[1, :, PACK - 1, cols])
-        w_planes[1, PACK - 1] = last_plane[:]
+        load_planes(1, PACK - 1, 1, "v_scale_table")
         for h in range(2):
             interleave(nc.scalar.copy, w_grouped[0][h][:], w_picked[:, :, half_slots[h]])
         pick_in_place(2, 0)
-        third_picked = sb("third_picked", [P, HALF], F32)
-        nc.vector.tensor_copy(third_picked[:], w_planes[1, 2].indirect(half_lists[1]))
-        nc.scalar.copy(out=w_grouped[1][1][:, :, 2], in_=third_picked[:])
+        pair_picked = sb("pair_picked", [P, 2, HALF], BF16)
+        nc.scalar.activation(pair_picked[:, 0, :], w_planes[1, 2].indirect(half_lists[1]), COPY)
         load_xm(2, "w_picked")
         for h in range(2):
             pick_in_place(0, h)
-        row_weights = sb("row_weights", [P, PACK], F32, "third_picked")
+        row_weights = sb("row_weights", [P, PACK], F32, "w_planes0_0")
         nc.sync.dma_start(row_weights[:], wt[0].rearrange("(p j) o -> p (j o)", j=PACK))
         student_pass(0, 0, "v_table")
         load_xm(2, "w_grouped0_0")
@@ -230,19 +224,17 @@ def tile_attend_gds_nce_kernel(tc, xT, wT, v_words, v_scales, wt, xm, offs, out)
         student_pass(0, 1, "x_grouped1")
         load_xm(4, "w_grouped0_1")
 
-        last_rounded = sb("last_rounded", [P, T], BF16)
-        for cols in pieces:
-            nc.scalar.activation(last_rounded[:, cols], last_plane[:, cols], COPY)
         pick_in_place(PACK - 1, 0)
         student_pass(1, 0, None)
-        nc.scalar.activation(w_grouped[1][1][:, :, PACK - 1], last_rounded[:].indirect(half_lists[1]), COPY)
+        nc.scalar.activation(pair_picked[:, 1, :], w_planes[1, PACK - 1].indirect(half_lists[1]), COPY)
+        nc.scalar.copy(out=w_grouped[1][1][:, :, 2:PACK], in_=pair_picked[:].rearrange("p t s -> p s t"))
         student_pass(1, 1, None)
 
         xm_codes, xm_scales = {}, {}
 
         def lay_out_xm(first, count, grouped, copy):
-            for u in range(count):
-                interleave(copy, grouped[:, u * P : (u + 1) * P, :], xm_raw[first + u])
+            raw, column = xm_raw[first]
+            interleave(copy, grouped[:], raw[:, :, column : column + count * P])
 
         def quantize_xm(first, count, grouped, scales=None):
             codes = sb("xm_codes%d" % first, [P, count * P], U32)
@@ -264,7 +256,7 @@ def tile_attend_gds_nce_kernel(tc, xT, wT, v_words, v_scales, wt, xm, offs, out)
                 stop=True,
             )
 
-        even_area, odd_area, last_g_area = 0, 3 * KIB, 7 * KIB
+        half_areas, g_areas = (0, 4 * KIB), {2: 8 * KIB, 3: 9 * KIB}
 
         grouped = sb("xm_grouped0", [P, 2 * P, PACK], BF16, "w_grouped1_1")
         lay_out_xm(0, 2, grouped, nc.vector.tensor_copy)
@@ -272,10 +264,10 @@ def tile_attend_gds_nce_kernel(tc, xT, wT, v_words, v_scales, wt, xm, offs, out)
 
         for q in range(SLOT_TILES):
             tanh_and_turn("student", q, score_banks[q], 0.5, False)
-            if q < SLOT_TILES - 1:
+            if q not in g_areas:
                 g_grouped = sb("g_grouped%d" % q, [P, P, PACK], BF16)
             else:
-                g_grouped = staged("g_grouped%d" % q, [P, P, PACK], BF16, last_g_area)
+                g_grouped = staged("g_grouped%d" % q, [P, P, PACK], BF16, g_areas[q])
             nc.vector.scalar_tensor_tensor(
                 g_grouped[:],
                 diff_banks[q][:].rearrange("p (j s) -> p s j", j=PACK),
@@ -291,52 +283,50 @@ def tile_attend_gds_nce_kernel(tc, xT, wT, v_words, v_scales, wt, xm, offs, out)
         for window in windows:
             nc.vector.memset(window[:], 0.0)
 
-        def result_tile(m):
-            area = odd_area if m % 2 else even_area
-            return staged("dw%d" % m, [P, N], F32, area + (m // 2 % 2) * KIB)
+        half_banks = (score_banks, diff_banks)
+        half_copies = (nc.scalar.copy, nc.vector.tensor_copy)
+        shared_slot = (0, 1)
+        results = {}
 
-        def scatter_and_store(m, dw):
-            window = windows[m % WINDOWS]
-            if m % 2:
-                nc.vector.tensor_copy(window[:].indirect(offsets[:]), dw[:])
+        def fetch(m, h):
+            bank = half_banks[h][m % SLOT_TILES][:, :HALF]
+            gradient_product(m, bank, half_slots[h])
+            if m % 2 != shared_slot[h]:
+                at = 3 * KIB
             else:
+                at = KIB // 2 if m < 4 else 0
+            results[m, h] = staged("dw%d_%d" % (m, h), [P, HALF], F32, half_areas[h] + at)
+            half_copies[h](out=results[m, h][:], in_=bank)
+
+        def scatter(m, h):
+            window = windows[m % WINDOWS]
+            if h == 0:
+                nc.scalar.activation(window[:].indirect(half_lists[h]), results[m, h][:], COPY)
+            else:
+                nc.vector.tensor_copy(window[:].indirect(half_lists[h]), results[m, h][:])
+                nc.sync.dma_start(out[m * P : (m + 1) * P, :], window[:])
+
+        def finish_pair(first):
+            for h in range(2):
+                for m in (first, first + 1):
+                    fetch(m, h)
+            for m in (first, first + 1):
                 for h in range(2):
-                    nc.scalar.activation(window[:].indirect(half_lists[h]), dw[:, half_slots[h]], COPY)
-            nc.sync.dma_start(out[m * P : (m + 1) * P, :], window[:])
+                    scatter(m, h)
 
-        def finish(m):
-            bank = score_banks[(m + 1) % SLOT_TILES]
-            gradient_product(m, bank[:], slice(0, N))
-            dw = result_tile(m)
-            copy = nc.vector.tensor_copy if m % 2 else nc.scalar.copy
-            copy(out=dw[:], in_=bank[:])
-            scatter_and_store(m, dw)
-
-        dw = result_tile(0)
-        for h, copy in enumerate((nc.scalar.copy, nc.vector.tensor_copy)):
-            gradient_product(0, score_banks[h][:, :HALF], half_slots[h])
-            copy(out=dw[:, half_slots[h]], in_=score_banks[h][:, :HALF])
-        scatter_and_store(0, dw)
-
+        finish_pair(0)
         grouped = sb("xm_grouped2", [P, 2 * P, PACK], BF16, "student_tanh2")
         lay_out_xm(2, 2, grouped, nc.scalar.copy)
-        quantize_xm(2, 2, grouped, staged("xm_scales2", [P, 2 * P], U8, last_g_area))
-        grouped = staged("xm_grouped4", [P, P, PACK], BF16, last_g_area + 2 * P)
-        lay_out_xm(4, 1, grouped, nc.vector.tensor_copy)
-        finish(1)
-        quantize_xm(4, 1, grouped)
-        finish(2)
-        grouped = staged("xm_grouped5", [P, P, PACK], BF16, odd_area)
-        lay_out_xm(5, 1, grouped, nc.vector.tensor_copy)
-        finish(3)
-        quantize_xm(5, 1, grouped)
-        grouped = staged("xm_grouped6", [P, P, PACK], BF16, even_area + 2 * KIB)
+        quantize_xm(2, 2, grouped, staged("xm_scales2", [P, 2 * P], U8, g_areas[2]))
+        grouped = staged("xm_grouped4", [P, 2 * P, PACK], BF16, g_areas[3])
+        lay_out_xm(4, 2, grouped, nc.vector.tensor_copy)
+        quantize_xm(4, 2, grouped)
+        finish_pair(2)
+        finish_pair(4)
+        grouped = staged("xm_grouped6", [P, P, PACK], BF16, half_areas[0] + KIB)
         lay_out_xm(6, 1, grouped, nc.scalar.copy)
-        finish(4)
-        quantize_xm(6, 1, grouped, staged("xm_scales6", [P, P], U8, odd_area + 2 * KIB))
-        grouped = staged("xm_grouped7", [P, P, PACK], BF16, odd_area + 2 * KIB + P)
+        quantize_xm(6, 1, grouped, staged("xm_scales6", [P, P], U8, half_areas[1] + KIB))
+        grouped = staged("xm_grouped7", [P, P, PACK], BF16, half_areas[1] + KIB + P)
         lay_out_xm(7, 1, grouped, nc.vector.tensor_copy)
-        finish(5)
         quantize_xm(7, 1, grouped)
-        finish(6)
-        finish(7)
+        finish_pair(6)

@@ -92,9 +92,12 @@ def tile_attend_gds_nce_kernel(tc, xT, wT, v_words, v_scales, wt, xm, offs, out)
             nc.sync.dma_start(raw[:], x_rows[g])
             return raw
 
-        def load_xm(count, tag):
+        def load_xm(count, tag, at=None):
             first = len(xm_raw) * P
-            raw = sb("xm_raw%d" % len(xm_raw), [P, PACK, count * P], F32, tag)
+            if at is None:
+                raw = sb("xm_raw%d" % len(xm_raw), [P, PACK, count * P], F32, tag)
+            else:
+                raw = staged("xm_raw%d" % len(xm_raw), [P, PACK, count * P], F32, at)
             nc.sync.dma_start(raw[:], xm_rows[:, :, first : first + count * P])
             xm_raw.extend((raw, u * P) for u in range(count))
 
@@ -131,7 +134,16 @@ def tile_attend_gds_nce_kernel(tc, xT, wT, v_words, v_scales, wt, xm, offs, out)
             x_scales.append(sb("x_scales%d" % g, [P, R], U8))
             quantize(nc, x_codes[g][:], x_scales[g][:], grouped[:], E4M3)
 
-        w_grouped = [[sb("w_grouped%d_%d" % (g, h), [P, HALF, PACK], BF16) for h in range(2)] for g in range(PASSES)]
+        second_area = 4 * KIB
+        w_grouped = [
+            [
+                staged("w_grouped0_1", [P, HALF, PACK], BF16, second_area)
+                if (g, h) == (0, 1)
+                else sb("w_grouped%d_%d" % (g, h), [P, HALF, PACK], BF16)
+                for h in range(2)
+            ]
+            for g in range(PASSES)
+        ]
         w_picked = sb("w_picked", [P, PACK, N], F32)
 
         def pick_plane(t):
@@ -162,9 +174,13 @@ def tile_attend_gds_nce_kernel(tc, xT, wT, v_words, v_scales, wt, xm, offs, out)
                     stop=(g == PASSES - 1),
                 )
 
-        def tanh_and_turn(name, q, scores, scale, opens):
+        def tanh_and_turn(name, q, scores, scale, opens, parts=1):
             halves = sb("%s_tanh%d" % (name, q), [P, PACK, P], F32)
-            nc.scalar.activation(halves[:], scores[:].rearrange("p (j s) -> p j s", j=PACK), TANH, scale=scale)
+            step = PACK // parts
+            for j in range(0, PACK, step):
+                nc.scalar.activation(
+                    halves[:, j : j + step, :].rearrange("p j s -> p (j s)"), scores[:, j * P : (j + step) * P], TANH, scale=scale
+                )
             for j in range(PACK):
                 nc.tensor.matmul(
                     diff_banks[q][:, j * P : (j + 1) * P],
@@ -222,13 +238,18 @@ def tile_attend_gds_nce_kernel(tc, xT, wT, v_words, v_scales, wt, xm, offs, out)
         for h in range(2):
             pick_in_place(1, h)
         student_pass(0, 1, "x_grouped1")
-        load_xm(4, "w_grouped0_1")
+        load_xm(2, None, second_area)
 
         pick_in_place(PACK - 1, 0)
         student_pass(1, 0, None)
-        nc.scalar.activation(pair_picked[:, 1, :], w_planes[1, PACK - 1].indirect(half_lists[1]), COPY)
-        nc.scalar.copy(out=w_grouped[1][1][:, :, 2:PACK], in_=pair_picked[:].rearrange("p t s -> p s t"))
+        for u in range(2):
+            tile_list = offsets[:, (2 + u) * (P // 16) : (3 + u) * (P // 16)]
+            nc.scalar.activation(pair_picked[:, 1, u * P : (u + 1) * P], w_planes[1, PACK - 1].indirect(tile_list), COPY)
+        for u in range(2):
+            cols = slice(u * P, (u + 1) * P)
+            nc.scalar.copy(out=w_grouped[1][1][:, cols, 2:PACK], in_=pair_picked[:, :, cols].rearrange("p t s -> p s t"))
         student_pass(1, 1, None)
+        load_xm(2, "pair_picked")
 
         xm_codes, xm_scales = {}, {}
 
@@ -256,14 +277,14 @@ def tile_attend_gds_nce_kernel(tc, xT, wT, v_words, v_scales, wt, xm, offs, out)
                 stop=True,
             )
 
-        half_areas, g_areas = (0, 4 * KIB), {2: 8 * KIB, 3: 9 * KIB}
+        half_areas, g_areas = (0, second_area), {2: 8 * KIB, 3: 9 * KIB}
 
         grouped = sb("xm_grouped0", [P, 2 * P, PACK], BF16, "w_grouped1_1")
         lay_out_xm(0, 2, grouped, nc.vector.tensor_copy)
         quantize_xm(0, 2, grouped)
 
         for q in range(SLOT_TILES):
-            tanh_and_turn("student", q, score_banks[q], 0.5, False)
+            tanh_and_turn("student", q, score_banks[q], 0.5, False, 2)
             if q not in g_areas:
                 g_grouped = sb("g_grouped%d" % q, [P, P, PACK], BF16)
             else:
@@ -285,18 +306,18 @@ def tile_attend_gds_nce_kernel(tc, xT, wT, v_words, v_scales, wt, xm, offs, out)
 
         half_banks = (score_banks, diff_banks)
         half_copies = (nc.scalar.copy, nc.vector.tensor_copy)
-        shared_slot = (0, 1)
+        result_at = ((1, 5, 1, 5, 0, 5, 4, 6), (6, 2, 6, 2, 6, 1, 0, 2))
         results = {}
 
         def fetch(m, h):
-            bank = half_banks[h][m % SLOT_TILES][:, :HALF]
-            gradient_product(m, bank, half_slots[h])
-            if m % 2 != shared_slot[h]:
-                at = 3 * KIB
-            else:
-                at = KIB // 2 if m < 4 else 0
+            at = result_at[h][m] * KIB // 2
             results[m, h] = staged("dw%d_%d" % (m, h), [P, HALF], F32, half_areas[h] + at)
-            half_copies[h](out=results[m, h][:], in_=bank)
+            parts = 2 if (m, h) == (0, 0) else 1
+            width = HALF // parts
+            for u in range(parts):
+                bank = half_banks[h][(m + 2 * u) % SLOT_TILES][:, :width]
+                gradient_product(m, bank, slice(h * HALF + u * width, h * HALF + (u + 1) * width))
+                half_copies[h](out=results[m, h][:, u * width : (u + 1) * width], in_=bank)
 
         def scatter(m, h):
             window = windows[m % WINDOWS]
@@ -314,19 +335,16 @@ def tile_attend_gds_nce_kernel(tc, xT, wT, v_words, v_scales, wt, xm, offs, out)
                 for h in range(2):
                     scatter(m, h)
 
-        finish_pair(0)
         grouped = sb("xm_grouped2", [P, 2 * P, PACK], BF16, "student_tanh2")
         lay_out_xm(2, 2, grouped, nc.scalar.copy)
         quantize_xm(2, 2, grouped, staged("xm_scales2", [P, 2 * P], U8, g_areas[2]))
         grouped = staged("xm_grouped4", [P, 2 * P, PACK], BF16, g_areas[3])
         lay_out_xm(4, 2, grouped, nc.vector.tensor_copy)
+        finish_pair(0)
         quantize_xm(4, 2, grouped)
         finish_pair(2)
         finish_pair(4)
-        grouped = staged("xm_grouped6", [P, P, PACK], BF16, half_areas[0] + KIB)
-        lay_out_xm(6, 1, grouped, nc.scalar.copy)
-        quantize_xm(6, 1, grouped, staged("xm_scales6", [P, P], U8, half_areas[1] + KIB))
-        grouped = staged("xm_grouped7", [P, P, PACK], BF16, half_areas[1] + KIB + P)
-        lay_out_xm(7, 1, grouped, nc.vector.tensor_copy)
-        quantize_xm(7, 1, grouped)
+        grouped = staged("xm_grouped6", [P, 2 * P, PACK], BF16, g_areas[3])
+        lay_out_xm(6, 2, grouped, nc.gpsimd.tensor_copy)
+        quantize_xm(6, 2, grouped, staged("xm_scales6", [P, 2 * P], U8, half_areas[1] + 3 * KIB // 2))
         finish_pair(6)

@@ -229,14 +229,16 @@ def tile_attend_gds_nce_kernel(tc, xT, wT, v_words, v_scales, wt, xm, offs, out)
         pair_picked = sb("pair_picked", [P, 2, HALF], BF16)
         nc.scalar.activation(pair_picked[:, 0, :], w_planes[1, 2].indirect(half_lists[1]), COPY)
         load_xm(2, "w_picked")
-        for h in range(2):
-            pick_in_place(0, h)
+        low_picked = sb("low_picked", [P, 2, HALF], BF16)
+        pick_in_place(0, 0)
+        nc.scalar.activation(low_picked[:, 0, :], w_planes[1, 0].indirect(half_lists[1]), COPY)
         row_weights = sb("row_weights", [P, PACK], F32, "w_planes0_0")
         nc.sync.dma_start(row_weights[:], wt[0].rearrange("(p j) o -> p (j o)", j=PACK))
         student_pass(0, 0, "v_table")
         load_xm(2, "w_grouped0_0")
-        for h in range(2):
-            pick_in_place(1, h)
+        pick_in_place(1, 0)
+        nc.scalar.activation(low_picked[:, 1, :], w_planes[1, 1].indirect(half_lists[1]), COPY)
+        nc.scalar.copy(out=w_grouped[1][1][:, :, 0:2], in_=low_picked[:].rearrange("p t s -> p s t"))
         student_pass(0, 1, "x_grouped1")
         load_xm(2, None, second_area)
 
@@ -306,7 +308,7 @@ def tile_attend_gds_nce_kernel(tc, xT, wT, v_words, v_scales, wt, xm, offs, out)
 
         half_banks = (score_banks, diff_banks)
         half_copies = (nc.scalar.copy, nc.vector.tensor_copy)
-        result_at = ((1, 5, 1, 5, 0, 5, 4, 6), (6, 2, 6, 2, 6, 1, 0, 2))
+        result_at = ((0, 5, 0, 5, 0, 5, 4, 6), (6, 2, 6, 2, 6, 1, 0, 2))
         results = {}
 
         def fetch(m, h):
@@ -345,6 +347,6 @@ def tile_attend_gds_nce_kernel(tc, xT, wT, v_words, v_scales, wt, xm, offs, out)
         finish_pair(2)
         finish_pair(4)
         grouped = staged("xm_grouped6", [P, 2 * P, PACK], BF16, g_areas[3])
-        lay_out_xm(6, 2, grouped, nc.gpsimd.tensor_copy)
+        nc.gpsimd.tensor_copy(out=grouped[:], in_=xm_raw[6][0][:].rearrange("p t c -> p c t"))
         quantize_xm(6, 2, grouped, staged("xm_scales6", [P, 2 * P], U8, half_areas[1] + 3 * KIB // 2))
         finish_pair(6)

@@ -224,7 +224,7 @@ def tile_attend_gds_nce_kernel(tc, xT, wT, v_words, v_scales, wt, xm, offs, out)
             pick_plane(t)
         load_planes(1, PACK - 1, 1, "v_scale_table")
         for h in range(2):
-            interleave(nc.scalar.copy, w_grouped[0][h][:], w_picked[:, :, half_slots[h]])
+            interleave(nc.vector.tensor_copy, w_grouped[0][h][:], w_picked[:, :, half_slots[h]])
         pick_in_place(2, 0)
         pair_picked = sb("pair_picked", [P, 2, HALF], BF16)
         nc.scalar.activation(pair_picked[:, 0, :], w_planes[1, 2].indirect(half_lists[1]), COPY)

@@ -21,19 +21,19 @@ MULT = mybir.AluOpType.mult
 
 P = 128
 PACK = 4
-K_PASS = P * PACK
-PASSES = D // K_PASS
+PASSES = D // (P * PACK)
 HALF = N // 2
 SLOT_TILES = N // P
+OUT_TILES = D // P
 WINDOWS = 4
+RESULT_RING = 3
 KIB = 1024
-LOAD_TAGS = ("v_scale_table", "w_planes0_0", "v_table", "x_grouped1", "x_raw0", "x_raw1", "w_picked")
 
 
-def interleave(copy, grouped, raw):
+def weave(copy, grouped, planes):
     copy(
         out=grouped.rearrange("p (c i) t -> p c t i", i=PACK),
-        in_=raw.rearrange("p t (c i) -> p c t i", i=PACK),
+        in_=planes.rearrange("p t (c i) -> p c t i", i=PACK),
     )
 
 
@@ -44,142 +44,99 @@ def quantize(nc, codes, scales, grouped, fmt):
 def tile_attend_gds_nce_kernel(tc, xT, wT, v_words, v_scales, wt, xm, offs, out):
     nc = tc.nc
     with ExitStack() as ctx:
-        low = ctx.enter_context(tc.tile_pool(name="low", bufs=1))
-        loads = ctx.enter_context(tc.tile_pool(name="loads", bufs=1))
-        middle = ctx.enter_context(tc.tile_pool(name="middle", bufs=1))
         held = ctx.enter_context(tc.tile_pool(name="held", bufs=1))
-        high = ctx.enter_context(tc.tile_pool(name="high", bufs=1))
-        stage = ctx.enter_context(tc.tile_pool(name="stage", bufs=1))
+        first_area = ctx.enter_context(tc.tile_pool(name="first_area", bufs=1))
+        late_area = ctx.enter_context(tc.tile_pool(name="late_area", bufs=1))
+        result_area = ctx.enter_context(tc.tile_pool(name="result_area", bufs=1))
         psum = ctx.enter_context(tc.psum_pool(name="psum", bufs=1))
 
         def sb(name, shape, dtype, tag=None):
-            pool = loads if (tag or name) in LOAD_TAGS else held
-            return pool.tile(shape, dtype, name=name, tag=tag or name, align_bytes=64)
+            return held.tile(shape, dtype, name=name, tag=tag or name, align_bytes=64)
 
-        def staged(name, shape, dtype, at):
-            return stage.tile(shape, dtype, name=name, align_bytes=64, offset=at)
+        def placed(pool, name, shape, dtype, at):
+            return pool.tile(shape, dtype, name=name, align_bytes=64, offset=at)
 
         offsets = held.tile([P, N // 16], U16, name="offsets")
-        half_lists = [offsets[:, h * (HALF // 16) : (h + 1) * (HALF // 16)] for h in range(2)]
-        half_slots = [slice(h * HALF, (h + 1) * HALF) for h in range(2)]
+
+        def listed(first, count):
+            return offsets[:, first // 16 : (first + count) // 16]
 
         diff_banks = [psum.tile([P, R], F32, name="diff_bank%d" % q) for q in range(SLOT_TILES)]
         score_banks = [psum.tile([P, R], F32, name="score_bank%d" % q) for q in range(SLOT_TILES)]
 
-        v_scale_table = sb("v_scale_table", [P, PASSES * T], U8)
-        nc.vector.memset(v_scale_table[:].bitcast(I32), 0)
-        v_slot_rows = sb("v_slot_rows", [P, PASSES * N], U8)
-        windows = [pool.tile([P, T], F32, name="window%d" % i) for i, pool in enumerate((low, middle, high))]
-        g_codes = sb("g_codes", [P, N], U32)
-        g_scales = sb("g_scales", [P, N], U8)
+        scale_table = sb("scale_table", [P, PASSES * T], U8)
+        nc.vector.memset(scale_table[:].bitcast(I32), 0)
         identity = sb("identity", [P, P], F32)
         make_identity(nc, identity[:])
 
-        w_rows = wT.rearrange("(g p t) c -> g p t c", p=P, t=PACK)
-        x_rows = xT[0].rearrange("(g p t) r -> g p t r", p=P, t=PACK)
-        xm_rows = xm[0].rearrange("(p t) d -> p t d", t=PACK)
-        w_planes = {}
-        xm_raw = []
-
-        def load_planes(g, first, count, tag=None):
-            planes = sb("w_planes%d_%d" % (g, first), [P, count * T], F32, tag)
-            nc.sync.dma_start(planes[:], w_rows[g, :, first : first + count, :].rearrange("p t c -> p (t c)"))
-            for u in range(count):
-                w_planes[g, first + u] = planes[:, u * T : (u + 1) * T]
-
-        def load_x(g):
-            raw = sb("x_raw%d" % g, [P, PACK, R], F32)
-            nc.sync.dma_start(raw[:], x_rows[g])
-            return raw
-
-        def load_xm(count, tag, at=None):
-            first = len(xm_raw) * P
-            if at is None:
-                raw = sb("xm_raw%d" % len(xm_raw), [P, PACK, count * P], F32, tag)
-            else:
-                raw = staged("xm_raw%d" % len(xm_raw), [P, PACK, count * P], F32, at)
-            nc.sync.dma_start(raw[:], xm_rows[:, :, first : first + count * P])
-            xm_raw.extend((raw, u * P) for u in range(count))
-
-        x_raw = [load_x(0)]
+        w_rows = wT.rearrange("(g p t) c -> g p (t c)", p=P, t=PACK)
+        x_raw = sb("x_raw", [P, PASSES, PACK * R], F32)
+        nc.sync.dma_start(x_raw[:], xT[0].rearrange("(g p t) r -> p g (t r)", p=P, t=PACK))
         nc.sync.dma_start(offsets[:], offs)
         nc.sync.dma_start(
-            v_scale_table[0:P:8, :].bitcast(I32).rearrange("f (o t) -> f o t", o=PASSES),
+            scale_table[0:P:8, :].bitcast(I32).rearrange("f (o t) -> f o t", o=PASSES),
             v_scales.bitcast(I32).rearrange("o f t -> f o t"),
         )
-        load_planes(0, 0, 2)
-        x_raw.append(load_x(1))
         v_table = sb("v_table", [P, T], U32)
         nc.sync.dma_start(v_table[:].bitcast(I32), v_words[0].rearrange("p t b -> p (t b)").bitcast(I32))
+        w_first = placed(first_area, "w_first", [P, PACK * T], F32, 0)
+        nc.sync.dma_start(w_first[:], w_rows[0])
 
-        v_picked_scales = sb("v_picked_scales", [P, PASSES * N], U8)
+        picked_scales = sb("picked_scales", [P, PASSES * N], U8)
         for g in range(PASSES):
-            nc.vector.tensor_copy(
-                v_picked_scales[:, g * N : (g + 1) * N], v_scale_table[:, g * T : (g + 1) * T].indirect(offsets[:])
-            )
-        nc.vector.tensor_copy(v_slot_rows[:].bitcast(I32), v_picked_scales[:].bitcast(I32))
+            nc.vector.tensor_copy(picked_scales[:, g * N : (g + 1) * N], scale_table[:, g * T : (g + 1) * T].indirect(offsets[:]))
+        v_scale_rows = sb("v_scale_rows", [P, PASSES * N], U8)
+        nc.vector.tensor_copy(v_scale_rows[:].bitcast(I32), picked_scales[:].bitcast(I32))
         for f in range(1, 4):
-            nc.sync.dma_start(v_slot_rows[f:P:32, :].bitcast(I32), v_picked_scales[8 * f : P : 32, :].bitcast(I32))
-        v_slot_scales = v_slot_rows[:].rearrange("p (o n) -> p o n", o=PASSES)
-        load_planes(0, 2, 2, "v_scale_table")
+            nc.sync.dma_start(v_scale_rows[f:P:32, :].bitcast(I32), picked_scales[8 * f : P : 32, :].bitcast(I32))
+        w_low = sb("w_low", [P, 2 * T], F32, "scale_table")
+        nc.sync.dma_start(w_low[:], w_rows[1][:, : 2 * T])
+
+        v_codes = []
+        for h in range(2):
+            v_pairs = sb("v_pairs%d" % h, [P, HALF], U32)
+            nc.vector.tensor_copy(v_pairs[:], v_table[:].indirect(listed(h * HALF, HALF)))
+            v_codes.append(sb("v_codes%d" % h, [P, PASSES, HALF], U16))
+            nc.vector.tensor_copy(v_codes[h][:], v_pairs[:].bitcast(U16).rearrange("p (n o) -> p o n", o=PASSES))
+        w_third = sb("w_third", [P, T], F32, "v_table")
+        nc.sync.dma_start(w_third[:], w_rows[1][:, 2 * T : 3 * T])
 
         x_codes, x_scales = [], []
         for g in range(PASSES):
             grouped = sb("x_grouped%d" % g, [P, R, PACK], BF16)
             nc.scalar.copy(
                 out=grouped[:].rearrange("p (j s) t -> p s t j", j=PACK),
-                in_=x_raw[g][:].rearrange("p t (s j) -> p s t j", j=PACK),
+                in_=x_raw[:, g, :].rearrange("p (t s j) -> p s t j", t=PACK, j=PACK),
             )
             x_codes.append(sb("x_codes%d" % g, [P, R], U32))
             x_scales.append(sb("x_scales%d" % g, [P, R], U8))
             quantize(nc, x_codes[g][:], x_scales[g][:], grouped[:], E4M3)
+        w_last = sb("w_last", [P, T], F32, "x_raw")
+        nc.sync.dma_start(w_last[:], w_rows[1][:, 3 * T :])
 
-        second_area = 4 * KIB
-        w_grouped = [
-            [
-                staged("w_grouped0_1", [P, HALF, PACK], BF16, second_area)
-                if (g, h) == (0, 1)
-                else sb("w_grouped%d_%d" % (g, h), [P, HALF, PACK], BF16)
-                for h in range(2)
-            ]
-            for g in range(PASSES)
-        ]
-        w_picked = sb("w_picked", [P, PACK, N], F32)
+        windows = [sb("window%d" % i, [P, T], F32) for i in range(WINDOWS)]
+        for window in windows:
+            nc.vector.memset(window[:], 0.0)
 
-        def pick_plane(t):
-            if t < 2:
-                nc.scalar.activation(w_picked[:, t, :], w_planes[0, t].indirect(offsets[:]), COPY)
-            else:
-                nc.vector.tensor_copy(w_picked[:, t, :], w_planes[0, t].indirect(offsets[:]))
+        def score_pass(q, codes, scales, fmt, g):
+            nc.tensor.matmul_mx(
+                out=score_banks[q][:],
+                lhsT=codes.bitcast(fmt),
+                lhsT_scale=scales,
+                rhs=x_codes[g][:].bitcast(E4M3),
+                rhs_scale=x_scales[g][:],
+                start=(g == 0),
+                stop=(g == PASSES - 1),
+            )
 
-        def pick_in_place(t, h):
-            nc.vector.tensor_copy(w_grouped[1][h][:, :, t], w_planes[1, t].indirect(half_lists[h]))
-
-        def student_pass(g, h, tag):
-            codes = sb("w_codes%d_%d" % (g, h), [P, HALF], U32, tag)
-            scales = sb("w_scales%d_%d" % (g, h), [P, HALF], U8)
-            if g == 0:
-                quantize(nc, codes[:], scales[:], w_grouped[g][h][:], E4M3)
-            for u in range(2):
-                cols = slice(u * P, (u + 1) * P)
-                if g == 1:
-                    quantize(nc, codes[:, cols], scales[:, cols], w_grouped[g][h][:, cols, :], E4M3)
-                nc.tensor.matmul_mx(
-                    out=score_banks[2 * h + u][:],
-                    lhsT=codes[:, cols].bitcast(E4M3),
-                    lhsT_scale=scales[:, cols],
-                    rhs=x_codes[g][:].bitcast(E4M3),
-                    rhs_scale=x_scales[g][:],
-                    start=(g == 0),
-                    stop=(g == PASSES - 1),
-                )
-
-        def tanh_and_turn(name, q, scores, scale, opens, parts=1):
-            halves = sb("%s_tanh%d" % (name, q), [P, PACK, P], F32)
+        def tanh_and_turn(q, halves, scale, opens, parts):
             step = PACK // parts
             for j in range(0, PACK, step):
                 nc.scalar.activation(
-                    halves[:, j : j + step, :].rearrange("p j s -> p (j s)"), scores[:, j * P : (j + step) * P], TANH, scale=scale
+                    halves[:, j : j + step, :].rearrange("p j s -> p (j s)"),
+                    score_banks[q][:, j * P : (j + step) * P],
+                    TANH,
+                    scale=scale,
                 )
             for j in range(PACK):
                 nc.tensor.matmul(
@@ -191,108 +148,104 @@ def tile_attend_gds_nce_kernel(tc, xT, wT, v_words, v_scales, wt, xm, offs, out)
                     stop=(not opens and j == PACK - 1),
                 )
 
-        def teacher():
-            v_codes = []
-            for h in range(2):
-                v_pairs = sb("v_pairs%d" % h, [P, HALF], U32)
-                nc.vector.tensor_copy(v_pairs[:], v_table[:].indirect(half_lists[h]))
-                v_codes.append(sb("v_codes%d" % h, [P, PASSES, HALF], U16))
-                nc.vector.tensor_copy(v_codes[h][:], v_pairs[:].bitcast(U16).rearrange("p (n o) -> p o n", o=PASSES))
-            for q in range(SLOT_TILES):
-                cols = slice(q * P, (q + 1) * P)
-                half_cols = slice((q % 2) * P, (q % 2 + 1) * P)
-                for g in range(PASSES):
-                    nc.tensor.matmul_mx(
-                        out=score_banks[q][:],
-                        lhsT=v_codes[q // 2][:, g, half_cols].bitcast(E2M1),
-                        lhsT_scale=v_slot_scales[:, g, cols],
-                        rhs=x_codes[g][:].bitcast(E4M3),
-                        rhs_scale=x_scales[g][:],
-                        start=(g == 0),
-                        stop=(g == PASSES - 1),
-                    )
-            for q in range(SLOT_TILES):
-                tanh_and_turn("teacher", q, score_banks[q], -0.5, True)
+        for q in range(SLOT_TILES):
+            for g in range(PASSES):
+                within = slice((q % 2) * P, (q % 2 + 1) * P)
+                score_pass(q, v_codes[q // 2][:, g, within], v_scale_rows[:, g * N + q * P : g * N + (q + 1) * P], E2M1, g)
+        for q in range(SLOT_TILES):
+            tanh_and_turn(q, sb("teacher_tanh%d" % q, [P, PACK, P], F32), -0.5, True, 1)
 
-        for t in range(2):
-            pick_plane(t)
-        load_planes(1, 2, 1, "w_planes0_0")
-        teacher()
-        load_planes(1, 0, 1, "v_table")
-        load_planes(1, 1, 1, "x_grouped1")
-        for t in range(2, PACK):
-            pick_plane(t)
-        load_planes(1, PACK - 1, 1, "v_scale_table")
+        w_picked = sb("w_picked", [P, PACK, N], F32)
+        for t in range(PACK):
+            plane = w_first[:, t * T : (t + 1) * T].indirect(offsets[:])
+            if t < 2:
+                nc.scalar.activation(w_picked[:, t, :], plane, COPY)
+            else:
+                nc.vector.tensor_copy(w_picked[:, t, :], plane)
+        w_grouped = [
+            [
+                placed(late_area, "w_grouped1_1", [P, HALF, PACK], BF16, KIB)
+                if (g, h) == (1, 1)
+                else sb("w_grouped%d_%d" % (g, h), [P, HALF, PACK], BF16)
+                for h in range(2)
+            ]
+            for g in range(PASSES)
+        ]
         for h in range(2):
-            interleave(nc.vector.tensor_copy, w_grouped[0][h][:], w_picked[:, :, half_slots[h]])
-        pick_in_place(2, 0)
-        pair_picked = sb("pair_picked", [P, 2, HALF], BF16)
-        nc.scalar.activation(pair_picked[:, 0, :], w_planes[1, 2].indirect(half_lists[1]), COPY)
-        load_xm(2, "w_picked")
-        low_picked = sb("low_picked", [P, 2, HALF], BF16)
-        pick_in_place(0, 0)
-        nc.scalar.activation(low_picked[:, 0, :], w_planes[1, 0].indirect(half_lists[1]), COPY)
-        row_weights = sb("row_weights", [P, PACK], F32, "w_planes0_0")
-        nc.sync.dma_start(row_weights[:], wt[0].rearrange("(p j) o -> p (j o)", j=PACK))
-        student_pass(0, 0, "v_table")
-        load_xm(2, "w_grouped0_0")
-        pick_in_place(1, 0)
-        nc.scalar.activation(low_picked[:, 1, :], w_planes[1, 1].indirect(half_lists[1]), COPY)
-        nc.scalar.copy(out=w_grouped[1][1][:, :, 0:2], in_=low_picked[:].rearrange("p t s -> p s t"))
-        student_pass(0, 1, "x_grouped1")
-        load_xm(2, None, second_area)
+            weave(nc.vector.tensor_copy, w_grouped[0][h][:], w_picked[:, :, h * HALF : (h + 1) * HALF])
 
-        pick_in_place(PACK - 1, 0)
-        student_pass(1, 0, None)
+        xm_rows = xm[0].rearrange("(p t) d -> p t d", t=PACK)
+        xm_raw = []
+        for pair in range(OUT_TILES // 2):
+            raw = placed(first_area, "xm_raw%d" % pair, [P, PACK, 2 * P], F32, pair * 4 * KIB)
+            nc.sync.dma_start(raw[:], xm_rows[:, :, pair * 2 * P : (pair + 1) * 2 * P])
+            xm_raw.append(raw)
+            if pair == 0:
+                row_weights = placed(first_area, "row_weights", [P, PACK], F32, 16 * KIB)
+                nc.sync.dma_start(row_weights[:], wt[0].rearrange("(p j) o -> p (j o)", j=PACK))
+
+        def first_pass(h, tag):
+            codes = sb("w_codes0_%d" % h, [P, HALF], U32, tag)
+            scales = sb("w_scales0_%d" % h, [P, HALF], U8)
+            quantize(nc, codes[:], scales[:], w_grouped[0][h][:], E4M3)
+            for u in range(2):
+                cols = slice(u * P, (u + 1) * P)
+                score_pass(2 * h + u, codes[:, cols], scales[:, cols], E4M3, 0)
+
+        def last_pass(h):
+            codes = sb("w_codes1_%d" % h, [P, HALF], U32)
+            scales = sb("w_scales1_%d" % h, [P, HALF], U8)
+            for u in range(2):
+                cols = slice(u * P, (u + 1) * P)
+                quantize(nc, codes[:, cols], scales[:, cols], w_grouped[1][h][:, cols, :], E4M3)
+                score_pass(2 * h + u, codes[:, cols], scales[:, cols], E4M3, 1)
+
+        low_picked = sb("low_picked", [P, 2, HALF], F32)
+        for t in range(2):
+            plane = w_low[:, t * T : (t + 1) * T]
+            nc.vector.tensor_copy(w_grouped[1][0][:, :, t], plane.indirect(listed(0, HALF)))
+            nc.scalar.activation(low_picked[:, t, :], plane.indirect(listed(HALF, HALF)), COPY)
+        nc.scalar.copy(out=w_grouped[1][1][:, :, 0:2], in_=low_picked[:].rearrange("p t s -> p s t"))
+        first_pass(0, "scale_table")
+        high_picked = sb("high_picked", [P, 2, HALF], BF16)
+        nc.vector.tensor_copy(w_grouped[1][0][:, :, 2], w_third[:].indirect(listed(0, HALF)))
+        nc.scalar.activation(high_picked[:, 0, :], w_third[:].indirect(listed(HALF, HALF)), COPY)
+        first_pass(1, "v_table")
+        nc.vector.tensor_copy(w_grouped[1][0][:, :, 3], w_last[:].indirect(listed(0, HALF)))
+        last_pass(0)
         for u in range(2):
-            tile_list = offsets[:, (2 + u) * (P // 16) : (3 + u) * (P // 16)]
-            nc.scalar.activation(pair_picked[:, 1, u * P : (u + 1) * P], w_planes[1, PACK - 1].indirect(tile_list), COPY)
+            nc.scalar.activation(high_picked[:, 1, u * P : (u + 1) * P], w_last[:].indirect(listed(HALF + u * P, P)), COPY)
         for u in range(2):
             cols = slice(u * P, (u + 1) * P)
-            nc.scalar.copy(out=w_grouped[1][1][:, cols, 2:PACK], in_=pair_picked[:, :, cols].rearrange("p t s -> p s t"))
-        student_pass(1, 1, None)
-        load_xm(2, "pair_picked")
+            nc.scalar.copy(out=w_grouped[1][1][:, cols, 2:PACK], in_=high_picked[:, :, cols].rearrange("p t s -> p s t"))
+        last_pass(1)
 
         xm_codes, xm_scales = {}, {}
 
-        def lay_out_xm(first, count, grouped, copy):
-            raw, column = xm_raw[first]
-            interleave(copy, grouped[:], raw[:, :, column : column + count * P])
-
-        def quantize_xm(first, count, grouped, scales=None):
+        def quantize_xm(first, count, grouped, scale_tile=None):
             codes = sb("xm_codes%d" % first, [P, count * P], U32)
-            if scales is None:
-                scales = sb("xm_scales%d" % first, [P, count * P], U8)
+            scales = scale_tile if scale_tile is not None else sb("xm_scales%d" % first, [P, count * P], U8)
             quantize(nc, codes[:], scales[:], grouped[:], E4M3)
             for u in range(count):
                 xm_codes[first + u] = codes[:, u * P : (u + 1) * P]
                 xm_scales[first + u] = scales[:, u * P : (u + 1) * P]
 
-        def gradient_product(m, bank, slots):
-            nc.tensor.matmul_mx(
-                out=bank,
-                lhsT=xm_codes[m].bitcast(E4M3),
-                lhsT_scale=xm_scales[m],
-                rhs=g_codes[:, slots].bitcast(E5M2),
-                rhs_scale=g_scales[:, slots],
-                start=True,
-                stop=True,
-            )
-
-        half_areas, g_areas = (0, second_area), {2: 8 * KIB, 3: 9 * KIB}
-
-        grouped = sb("xm_grouped0", [P, 2 * P, PACK], BF16, "w_grouped1_1")
-        lay_out_xm(0, 2, grouped, nc.vector.tensor_copy)
+        grouped = placed(late_area, "xm_grouped0", [P, 2 * P, PACK], BF16, KIB)
+        weave(nc.vector.tensor_copy, grouped[:], xm_raw[0][:])
         quantize_xm(0, 2, grouped)
+        second_grouped = placed(late_area, "xm_grouped2", [P, 2 * P, PACK], BF16, KIB)
+        nc.gpsimd.tensor_copy(out=second_grouped[:, P:, :], in_=xm_raw[1][:, :, P:].rearrange("p t c -> p c t"))
 
+        g_codes = sb("g_codes", [P, N], U32)
+        g_scales = sb("g_scales", [P, N], U8)
         for q in range(SLOT_TILES):
-            tanh_and_turn("student", q, score_banks[q], 0.5, False, 2)
-            if q not in g_areas:
-                g_grouped = sb("g_grouped%d" % q, [P, P, PACK], BF16)
+            tanh_and_turn(q, sb("student_tanh%d" % q, [P, PACK, P], F32), 0.5, False, 2)
+            if q == SLOT_TILES - 1:
+                g_grouped = sb("g_grouped3", [P, P, PACK], BF16)
             else:
-                g_grouped = staged("g_grouped%d" % q, [P, P, PACK], BF16, g_areas[q])
+                g_grouped = sb("g_grouped%d" % q, [P, P, PACK], BF16, "g_grouped%d" % (q % 2))
             nc.vector.scalar_tensor_tensor(
-                g_grouped[:],
+                g_grouped[:, :P, :],
                 diff_banks[q][:].rearrange("p (j s) -> p s j", j=PACK),
                 0.5,
                 row_weights[:].unsqueeze(1).to_broadcast([P, P, PACK]),
@@ -300,53 +253,52 @@ def tile_attend_gds_nce_kernel(tc, xT, wT, v_words, v_scales, wt, xm, offs, out)
                 MULT,
             )
             cols = slice(q * P, (q + 1) * P)
-            quantize(nc, g_codes[:, cols], g_scales[:, cols], g_grouped[:], E5M2)
+            quantize(nc, g_codes[:, cols], g_scales[:, cols], g_grouped[:, :P, :], E5M2)
 
-        windows.append(sb("window3", [P, T], F32, "x_raw0"))
-        for window in windows:
-            nc.vector.memset(window[:], 0.0)
+        weave(nc.scalar.copy, second_grouped[:, :P, :], xm_raw[1][:, :, :P])
+        quantize_xm(2, 2, second_grouped, sb("xm_scales2", [P, 2 * P], U8, "g_grouped0"))
+        late_grouped = {}
+        for first, at in ((4, 0), (6, 2 * KIB)):
+            late_grouped[first] = placed(late_area, "xm_grouped%d" % first, [P, 2 * P, PACK], BF16, at)
+            nc.gpsimd.tensor_copy(out=late_grouped[first][:], in_=xm_raw[first // 2][:].rearrange("p t c -> p c t"))
 
         half_banks = (score_banks, diff_banks)
         half_copies = (nc.scalar.copy, nc.vector.tensor_copy)
-        result_at = ((0, 5, 0, 5, 0, 5, 4, 6), (6, 2, 6, 2, 6, 1, 0, 2))
         results = {}
 
         def fetch(m, h):
-            at = result_at[h][m] * KIB // 2
-            results[m, h] = staged("dw%d_%d" % (m, h), [P, HALF], F32, half_areas[h] + at)
-            parts = 2 if (m, h) == (0, 0) else 1
+            if h == 0 and m >= 3:
+                results[m, h] = placed(result_area, "dw%d_0" % m, [P, HALF], F32, {3: 1, 4: 0, 5: 2, 6: 1, 7: 3}[m] * KIB // 2)
+            else:
+                results[m, h] = sb("dw%d_%d" % (m, h), [P, HALF], F32, "dw%d_%d" % ((m + m // 6) % RESULT_RING, h))
+            parts = 2 if m == 0 else 1
             width = HALF // parts
             for u in range(parts):
-                bank = half_banks[h][(m + 2 * u) % SLOT_TILES][:, :width]
-                gradient_product(m, bank, slice(h * HALF + u * width, h * HALF + (u + 1) * width))
+                bank = half_banks[h][(m % (4 - 2 * h) + 2 * u) % SLOT_TILES][:, :width]
+                slots = slice(h * HALF + u * width, h * HALF + (u + 1) * width)
+                nc.tensor.matmul_mx(
+                    out=bank,
+                    lhsT=xm_codes[m].bitcast(E4M3),
+                    lhsT_scale=xm_scales[m],
+                    rhs=g_codes[:, slots].bitcast(E5M2),
+                    rhs_scale=g_scales[:, slots],
+                    start=True,
+                    stop=True,
+                )
                 half_copies[h](out=results[m, h][:, u * width : (u + 1) * width], in_=bank)
 
-        def scatter(m, h):
+        def scatter(m):
             window = windows[m % WINDOWS]
-            if h == 0:
-                nc.scalar.activation(window[:].indirect(half_lists[h]), results[m, h][:], COPY)
-            else:
-                nc.vector.tensor_copy(window[:].indirect(half_lists[h]), results[m, h][:])
-                nc.sync.dma_start(out[m * P : (m + 1) * P, :], window[:])
+            nc.scalar.activation(window[:].indirect(listed(0, HALF)), results[m, 0][:], COPY)
+            nc.vector.tensor_copy(window[:].indirect(listed(HALF, HALF)), results[m, 1][:])
+            nc.sync.dma_start(out[m * P : (m + 1) * P, :], window[:])
 
-        def finish_pair(first):
-            for h in range(2):
-                for m in (first, first + 1):
-                    fetch(m, h)
-            for m in (first, first + 1):
+        for h in range(2):
+            fetch(0, h)
+        for m in range(OUT_TILES):
+            if m + 1 < OUT_TILES:
                 for h in range(2):
-                    scatter(m, h)
-
-        grouped = sb("xm_grouped2", [P, 2 * P, PACK], BF16, "student_tanh2")
-        lay_out_xm(2, 2, grouped, nc.scalar.copy)
-        quantize_xm(2, 2, grouped, staged("xm_scales2", [P, 2 * P], U8, g_areas[2]))
-        grouped = staged("xm_grouped4", [P, 2 * P, PACK], BF16, g_areas[3])
-        lay_out_xm(4, 2, grouped, nc.vector.tensor_copy)
-        finish_pair(0)
-        quantize_xm(4, 2, grouped)
-        finish_pair(2)
-        finish_pair(4)
-        grouped = staged("xm_grouped6", [P, 2 * P, PACK], BF16, g_areas[3])
-        nc.gpsimd.tensor_copy(out=grouped[:], in_=xm_raw[6][0][:].rearrange("p t c -> p c t"))
-        quantize_xm(6, 2, grouped, staged("xm_scales6", [P, 2 * P], U8, half_areas[1] + 3 * KIB // 2))
-        finish_pair(6)
+                    fetch(m + 1, h)
+            scatter(m)
+            if m in (0, 3):
+                quantize_xm(4 + 2 * (m // 3), 2, late_grouped[4 + 2 * (m // 3)])

from contextlib import ExitStack

import concourse.mybir as mybir
from concourse.masks import make_identity

D, T, N, R = 1024, 2048, 512, 512
FLOPS = 3 * 2 * D * N * R

F32 = mybir.dt.float32
BF16 = mybir.dt.bfloat16
I32 = mybir.dt.int32
U32 = mybir.dt.uint32
U16 = mybir.dt.uint16
U8 = mybir.dt.uint8
E4M3 = mybir.dt.float8_e4m3fn_x4
E5M2 = mybir.dt.float8_e5m2_x4
E2M1 = mybir.dt.float4_e2m1fn_x4
TANH = mybir.ActivationFunctionType.Tanh
COPY = mybir.ActivationFunctionType.Copy
MULT = mybir.AluOpType.mult

P = 128
PACK = 4
PASSES = D // (P * PACK)
HALF = N // 2
SLOT_TILES = N // P
OUT_TILES = D // P
WINDOWS = 4
RESULT_RING = 3
KIB = 1024


def weave(copy, grouped, planes):
    copy(
        out=grouped.rearrange("p (c i) t -> p c t i", i=PACK),
        in_=planes.rearrange("p t (c i) -> p c t i", i=PACK),
    )


def quantize(nc, codes, scales, grouped, fmt):
    nc.vector.quantize_mx(out=codes.bitcast(fmt), scales=scales, in_=grouped.rearrange("p c t -> p (c t)"))


def tile_attend_gds_nce_kernel(tc, xT, wT, v_words, v_scales, wt, xm, offs, out):
    nc = tc.nc
    with ExitStack() as ctx:
        held = ctx.enter_context(tc.tile_pool(name="held", bufs=1))
        first_area = ctx.enter_context(tc.tile_pool(name="first_area", bufs=1))
        late_area = ctx.enter_context(tc.tile_pool(name="late_area", bufs=1))
        result_area = ctx.enter_context(tc.tile_pool(name="result_area", bufs=1))
        psum = ctx.enter_context(tc.psum_pool(name="psum", bufs=1))

        def sb(name, shape, dtype, tag=None):
            return held.tile(shape, dtype, name=name, tag=tag or name, align_bytes=64)

        def placed(pool, name, shape, dtype, at):
            return pool.tile(shape, dtype, name=name, align_bytes=64, offset=at)

        offsets = held.tile([P, N // 16], U16, name="offsets")

        def listed(first, count):
            return offsets[:, first // 16 : (first + count) // 16]

        diff_banks = [psum.tile([P, R], F32, name="diff_bank%d" % q) for q in range(SLOT_TILES)]
        score_banks = [psum.tile([P, R], F32, name="score_bank%d" % q) for q in range(SLOT_TILES)]

        scale_table = sb("scale_table", [P, PASSES * T], U8)
        nc.vector.memset(scale_table[:].bitcast(I32), 0)
        identity = sb("identity", [P, P], F32)
        make_identity(nc, identity[:])

        w_rows = wT.rearrange("(g p t) c -> g p (t c)", p=P, t=PACK)
        x_raw = sb("x_raw", [P, PASSES, PACK * R], F32)
        nc.sync.dma_start(x_raw[:], xT[0].rearrange("(g p t) r -> p g (t r)", p=P, t=PACK))
        nc.sync.dma_start(offsets[:], offs)
        nc.sync.dma_start(
            scale_table[0:P:8, :].bitcast(I32).rearrange("f (o t) -> f o t", o=PASSES),
            v_scales.bitcast(I32).rearrange("o f t -> f o t"),
        )
        v_table = sb("v_table", [P, T], U32)
        nc.sync.dma_start(v_table[:].bitcast(I32), v_words[0].rearrange("p t b -> p (t b)").bitcast(I32))
        w_first = placed(first_area, "w_first", [P, PACK * T], F32, 0)
        nc.sync.dma_start(w_first[:], w_rows[0])

        picked_scales = sb("picked_scales", [P, PASSES * N], U8)
        for g in range(PASSES):
            nc.vector.tensor_copy(picked_scales[:, g * N : (g + 1) * N], scale_table[:, g * T : (g + 1) * T].indirect(offsets[:]))
        v_scale_rows = sb("v_scale_rows", [P, PASSES * N], U8)
        nc.vector.tensor_copy(v_scale_rows[:].bitcast(I32), picked_scales[:].bitcast(I32))
        for f in range(1, 4):
            nc.sync.dma_start(v_scale_rows[f:P:32, :].bitcast(I32), picked_scales[8 * f : P : 32, :].bitcast(I32))
        w_low = sb("w_low", [P, 2 * T], F32, "scale_table")
        nc.sync.dma_start(w_low[:], w_rows[1][:, : 2 * T])

        v_codes = []
        for h in range(2):
            v_pairs = sb("v_pairs%d" % h, [P, HALF], U32)
            nc.vector.tensor_copy(v_pairs[:], v_table[:].indirect(listed(h * HALF, HALF)))
            v_codes.append(sb("v_codes%d" % h, [P, PASSES, HALF], U16))
            nc.vector.tensor_copy(v_codes[h][:], v_pairs[:].bitcast(U16).rearrange("p (n o) -> p o n", o=PASSES))
        w_third = sb("w_third", [P, T], F32, "v_table")
        nc.sync.dma_start(w_third[:], w_rows[1][:, 2 * T : 3 * T])

        x_codes, x_scales = [], []
        for g in range(PASSES):
            grouped = sb("x_grouped%d" % g, [P, R, PACK], BF16)
            nc.scalar.copy(
                out=grouped[:].rearrange("p (j s) t -> p s t j", j=PACK),
                in_=x_raw[:, g, :].rearrange("p (t s j) -> p s t j", t=PACK, j=PACK),
            )
            x_codes.append(sb("x_codes%d" % g, [P, R], U32))
            x_scales.append(sb("x_scales%d" % g, [P, R], U8))
            quantize(nc, x_codes[g][:], x_scales[g][:], grouped[:], E4M3)
        w_last = sb("w_last", [P, T], F32, "x_raw")
        nc.sync.dma_start(w_last[:], w_rows[1][:, 3 * T :])

        windows = [sb("window%d" % i, [P, T], F32) for i in range(WINDOWS)]
        for window in windows:
            nc.vector.memset(window[:], 0.0)

        def score_pass(q, codes, scales, fmt, g):
            nc.tensor.matmul_mx(
                out=score_banks[q][:],
                lhsT=codes.bitcast(fmt),
                lhsT_scale=scales,
                rhs=x_codes[g][:].bitcast(E4M3),
                rhs_scale=x_scales[g][:],
                start=(g == 0),
                stop=(g == PASSES - 1),
            )

        def tanh_and_turn(q, halves, scale, opens, parts):
            step = PACK // parts
            for j in range(0, PACK, step):
                nc.scalar.activation(
                    halves[:, j : j + step, :].rearrange("p j s -> p (j s)"),
                    score_banks[q][:, j * P : (j + step) * P],
                    TANH,
                    scale=scale,
                )
            for j in range(PACK):
                nc.tensor.matmul(
                    diff_banks[q][:, j * P : (j + 1) * P],
                    lhsT=halves[:, j, :],
                    rhs=identity[:],
                    is_transpose=True,
                    start=(opens and j == 0),
                    stop=(not opens and j == PACK - 1),
                )

        for q in range(SLOT_TILES):
            for g in range(PASSES):
                within = slice((q % 2) * P, (q % 2 + 1) * P)
                score_pass(q, v_codes[q // 2][:, g, within], v_scale_rows[:, g * N + q * P : g * N + (q + 1) * P], E2M1, g)
        for q in range(SLOT_TILES):
            tanh_and_turn(q, sb("teacher_tanh%d" % q, [P, PACK, P], F32), -0.5, True, 1)

        w_picked = sb("w_picked", [P, PACK, N], F32)
        for t in range(PACK):
            plane = w_first[:, t * T : (t + 1) * T].indirect(offsets[:])
            if t < 2:
                nc.scalar.activation(w_picked[:, t, :], plane, COPY)
            else:
                nc.vector.tensor_copy(w_picked[:, t, :], plane)
        w_grouped = [
            [
                placed(late_area, "w_grouped1_1", [P, HALF, PACK], BF16, KIB)
                if (g, h) == (1, 1)
                else sb("w_grouped%d_%d" % (g, h), [P, HALF, PACK], BF16)
                for h in range(2)
            ]
            for g in range(PASSES)
        ]
        for h in range(2):
            weave(nc.vector.tensor_copy, w_grouped[0][h][:], w_picked[:, :, h * HALF : (h + 1) * HALF])

        xm_rows = xm[0].rearrange("(p t) d -> p t d", t=PACK)
        xm_raw = []
        for pair in range(OUT_TILES // 2):
            raw = placed(first_area, "xm_raw%d" % pair, [P, PACK, 2 * P], F32, pair * 4 * KIB)
            nc.sync.dma_start(raw[:], xm_rows[:, :, pair * 2 * P : (pair + 1) * 2 * P])
            xm_raw.append(raw)
            if pair == 0:
                row_weights = placed(first_area, "row_weights", [P, PACK], F32, 16 * KIB)
                nc.sync.dma_start(row_weights[:], wt[0].rearrange("(p j) o -> p (j o)", j=PACK))

        def first_pass(h, tag):
            codes = sb("w_codes0_%d" % h, [P, HALF], U32, tag)
            scales = sb("w_scales0_%d" % h, [P, HALF], U8)
            quantize(nc, codes[:], scales[:], w_grouped[0][h][:], E4M3)
            for u in range(2):
                cols = slice(u * P, (u + 1) * P)
                score_pass(2 * h + u, codes[:, cols], scales[:, cols], E4M3, 0)

        def last_pass(h):
            codes = sb("w_codes1_%d" % h, [P, HALF], U32)
            scales = sb("w_scales1_%d" % h, [P, HALF], U8)
            for u in range(2):
                cols = slice(u * P, (u + 1) * P)
                quantize(nc, codes[:, cols], scales[:, cols], w_grouped[1][h][:, cols, :], E4M3)
                score_pass(2 * h + u, codes[:, cols], scales[:, cols], E4M3, 1)

        low_picked = sb("low_picked", [P, 2, HALF], F32)
        for t in range(2):
            plane = w_low[:, t * T : (t + 1) * T]
            nc.vector.tensor_copy(w_grouped[1][0][:, :, t], plane.indirect(listed(0, HALF)))
            nc.scalar.activation(low_picked[:, t, :], plane.indirect(listed(HALF, HALF)), COPY)
        nc.scalar.copy(out=w_grouped[1][1][:, :, 0:2], in_=low_picked[:].rearrange("p t s -> p s t"))
        first_pass(0, "scale_table")
        high_picked = sb("high_picked", [P, 2, HALF], BF16)
        nc.vector.tensor_copy(w_grouped[1][0][:, :, 2], w_third[:].indirect(listed(0, HALF)))
        nc.scalar.activation(high_picked[:, 0, :], w_third[:].indirect(listed(HALF, HALF)), COPY)
        first_pass(1, "v_table")
        nc.vector.tensor_copy(w_grouped[1][0][:, :, 3], w_last[:].indirect(listed(0, HALF)))
        last_pass(0)
        for u in range(2):
            nc.scalar.activation(high_picked[:, 1, u * P : (u + 1) * P], w_last[:].indirect(listed(HALF + u * P, P)), COPY)
        for u in range(2):
            cols = slice(u * P, (u + 1) * P)
            nc.scalar.copy(out=w_grouped[1][1][:, cols, 2:PACK], in_=high_picked[:, :, cols].rearrange("p t s -> p s t"))
        last_pass(1)

        xm_codes, xm_scales = {}, {}

        def quantize_xm(first, count, grouped, scale_tile=None):
            codes = sb("xm_codes%d" % first, [P, count * P], U32)
            scales = scale_tile if scale_tile is not None else sb("xm_scales%d" % first, [P, count * P], U8)
            quantize(nc, codes[:], scales[:], grouped[:], E4M3)
            for u in range(count):
                xm_codes[first + u] = codes[:, u * P : (u + 1) * P]
                xm_scales[first + u] = scales[:, u * P : (u + 1) * P]

        grouped = placed(late_area, "xm_grouped0", [P, 2 * P, PACK], BF16, KIB)
        weave(nc.vector.tensor_copy, grouped[:], xm_raw[0][:])
        quantize_xm(0, 2, grouped)
        second_grouped = placed(late_area, "xm_grouped2", [P, 2 * P, PACK], BF16, KIB)
        nc.gpsimd.tensor_copy(out=second_grouped[:, P:, :], in_=xm_raw[1][:, :, P:].rearrange("p t c -> p c t"))

        g_codes = sb("g_codes", [P, N], U32)
        g_scales = sb("g_scales", [P, N], U8)
        for q in range(SLOT_TILES):
            tanh_and_turn(q, sb("student_tanh%d" % q, [P, PACK, P], F32), 0.5, False, 2)
            if q == SLOT_TILES - 1:
                g_grouped = sb("g_grouped3", [P, P, PACK], BF16)
            else:
                g_grouped = sb("g_grouped%d" % q, [P, P, PACK], BF16, "g_grouped%d" % (q % 2))
            nc.vector.scalar_tensor_tensor(
                g_grouped[:, :P, :],
                diff_banks[q][:].rearrange("p (j s) -> p s j", j=PACK),
                0.5,
                row_weights[:].unsqueeze(1).to_broadcast([P, P, PACK]),
                MULT,
                MULT,
            )
            cols = slice(q * P, (q + 1) * P)
            quantize(nc, g_codes[:, cols], g_scales[:, cols], g_grouped[:, :P, :], E5M2)

        weave(nc.scalar.copy, second_grouped[:, :P, :], xm_raw[1][:, :, :P])
        quantize_xm(2, 2, second_grouped, sb("xm_scales2", [P, 2 * P], U8, "g_grouped0"))
        late_grouped = {}
        for first, at in ((4, 0), (6, 2 * KIB)):
            late_grouped[first] = placed(late_area, "xm_grouped%d" % first, [P, 2 * P, PACK], BF16, at)
            nc.gpsimd.tensor_copy(out=late_grouped[first][:], in_=xm_raw[first // 2][:].rearrange("p t c -> p c t"))

        half_banks = (score_banks, diff_banks)
        half_copies = (nc.scalar.copy, nc.vector.tensor_copy)
        results = {}

        def fetch(m, h):
            if h == 0 and m >= 3:
                results[m, h] = placed(result_area, "dw%d_0" % m, [P, HALF], F32, {3: 1, 4: 0, 5: 2, 6: 1, 7: 3}[m] * KIB // 2)
            else:
                results[m, h] = sb("dw%d_%d" % (m, h), [P, HALF], F32, "dw%d_%d" % ((m + m // 6) % RESULT_RING, h))
            parts = 2 if m == 0 else 1
            width = HALF // parts
            for u in range(parts):
                bank = half_banks[h][(m % (4 - 2 * h) + 2 * u) % SLOT_TILES][:, :width]
                slots = slice(h * HALF + u * width, h * HALF + (u + 1) * width)
                nc.tensor.matmul_mx(
                    out=bank,
                    lhsT=xm_codes[m].bitcast(E4M3),
                    lhsT_scale=xm_scales[m],
                    rhs=g_codes[:, slots].bitcast(E5M2),
                    rhs_scale=g_scales[:, slots],
                    start=True,
                    stop=True,
                )
                half_copies[h](out=results[m, h][:, u * width : (u + 1) * width], in_=bank)

        def scatter(m):
            window = windows[m % WINDOWS]
            nc.scalar.activation(window[:].indirect(listed(0, HALF)), results[m, 0][:], COPY)
            nc.vector.tensor_copy(window[:].indirect(listed(HALF, HALF)), results[m, 1][:])
            nc.sync.dma_start(out[m * P : (m + 1) * P, :], window[:])

        for h in range(2):
            fetch(0, h)
        for m in range(OUT_TILES):
            if m + 1 < OUT_TILES:
                for h in range(2):
                    fetch(m + 1, h)
            scatter(m)
            if m in (0, 3):
                quantize_xm(4 + 2 * (m // 3), 2, late_grouped[4 + 2 * (m // 3)])
